import numpy as np, ml_dtypes
CORES = [3,7,11,15,131,135,139,143]
N = 8
import mx_ref
BF = ml_dtypes.bfloat16
def gcols(t, e):
    v = np.concatenate([t.reshape(8, 16, -1, 4), np.zeros((8, 16, 1, 4), BF)], axis=2)
    return np.ascontiguousarray(np.stack([v[g][:, e[g]] for g in range(8)])).reshape(128, -1)
def tile(rs):
    return np.stack(rs, axis=2).reshape(128, -1).astype(BF)
def pick(q, e):
    c = np.concatenate([q[0].reshape(128, -1, 4), np.zeros((128, 1, 4), np.uint8)], axis=1); s = np.concatenate([q[1], np.ones((16, 1), np.uint8)], axis=1)
    return (np.ascontiguousarray(c[:, e].reshape(128, -1)), np.ascontiguousarray(s[:, e]))
def join(*qs):
    return (np.concatenate([q[0] for q in qs], axis=1), np.concatenate([q[1] for q in qs], axis=1))
def put(q, e, v):
    c, s = q[0].reshape(128, -1, 4).copy(), q[1].copy(); c[:, e] = v[0].reshape(128, -1, 4); s[:, e] = v[1]
    return (c.reshape(128, -1), s)
def pk(c, s):
    return (np.ascontiguousarray(c), mx_ref.live(s))
def emit(q):
    return q[0], q[1]
def packed(v, rng):
    q = [mx_ref.quantize(np.ascontiguousarray(v[r])) for r in range(N)]
    return np.stack([a for a, b in q]), np.stack([mx_ref.plane(b, rng) for a, b in q])
def values_of_codes():
    e, c = np.zeros((128, 128, 4), np.float32), np.zeros((128, 2, 4), np.uint8)
    e[np.arange(128), np.arange(128), 0] = 1
    c[:127, :, 0] = np.arange(256).reshape(2, 128).T[:127]
    return mx_ref.matmul(mx_ref.quantize(e.reshape(128, 512).astype(BF)), (c.reshape(128, 8), np.full((16, 2), 127, np.uint8))).T.reshape(-1).astype(np.float64)
CODE_VALUE, SCALE_VALUE = values_of_codes(), 2.0 ** (np.arange(256) - 127.0)
def decode(q):
    return (CODE_VALUE[q[0]].reshape(16, 8, -1, 4) * SCALE_VALUE[q[1]][:, None, :, None] + 0.0).reshape(128, -1).astype(np.float32)
def f(rng, *shape):
    return mx_ref.flush((rng.standard_normal(shape, dtype=np.float32) * np.exp2(rng.integers(-2, 3, shape[:-1] + (1,)))).astype(BF))
def wide(rng, *shape, cols=0):
    v = rng.standard_normal(shape, dtype=np.float32) * np.exp2(rng.integers(-12, 13, shape)).astype(np.float32)
    if cols: v *= np.repeat(np.exp2(rng.integers(-cols, cols + 1, shape[:-2] + (1, shape[-1] // 4))) * (rng.random(shape[:-2] + (1, shape[-1] // 4)) > 0.0625), 4, axis=-1).astype(np.float32)
    return mx_ref.flush(v.astype(BF))
S, Z, E, C, A, R = 20, 16, 8, 320, 160, 3
DEPTH = np.arange(E)
AWAY = np.abs(np.arange(S)[:, None] - np.arange(S))
CONE = DEPTH[:, None, None] - AWAY[:, None, :, None] >= DEPTH
def cuts(p):
    rich = (p[::16] > 0).reshape(8, S, Z)[:, :, :E]
    good = 2 * np.sum(rich[:, None, None] & CONE, axis=(3, 4)) > np.sum(CONE, axis=(2, 3))
    return np.sum((good[:, :, :, None, None] & CONE).any(axis=(1, 2)), axis=2)
def slots(a):
    n = a[:, :, None]
    return np.where(DEPTH < n, Z * np.arange(S)[:, None] + n - 1 - DEPTH, -1).reshape(8, A)
def places(a, s):
    n, c, k = a[:, :, None], np.arange(S)[:, None], np.arange(Z)
    i = k - Z + n
    return np.where(i < 0, Z * c + k + n, np.where(i < s[:, :, None], C + E * c + i, Z * c + n - 1 - i)).reshape(8, C)
def big(v):
    v = v.astype(np.float32)
    v[np.abs(v) < np.float32(2.0 ** -16)] = 0
    return v.astype(BF)
def numbers_of(rng):
    return {"x": big(f(rng, N, 128, 4 * C)), "u": np.array(f(rng, N, 128, 512)), "v": np.array(f(rng, N, 128, 512))}
def weights(rng, still=[], fade=[]):
    w = big(f(rng, N, 128, 2048)).reshape(N, 8, 16, 4, 8, 16, 4)
    for i in still:
        w[:, :, i] = 0
        w[:, :, :, :, :, i] = 0
    for g in fade:
        w[:, g, 0, 0, g, 0, 0] = -64
        w[:, g, 0, 0, g, 1, 0] = 0.25
    c, p = packed(w.reshape(N, 128, 2048), rng)
    return {"wc": c, "ws": p}
def setup_inputs(rng):
    return {**numbers_of(rng), **weights(rng)}
def setup_inputs_zeros(rng):
    d = numbers_of(rng)
    x = d["x"].reshape(N, 8, 16, C, 4)
    x.transpose(0, 1, 3, 2, 4)[rng.permutation(N * 8 * C).reshape(N, 8, C) % 3 == 0] = 0
    for r in range(N): x[r][:, :, rng.permutation(C)[:C // 8]] = 0
    x[int(rng.integers(N))].reshape(8, 16, S, Z, 4)[:, :, :, :E] = 0
    return {"x": x.reshape(N, 128, 4 * C), "u": d["u"], "v": d["v"], **weights(rng)}
def setup_inputs_cones(rng):
    d = numbers_of(rng)
    x = d["x"].astype(np.float32).reshape(N, 8, 16, C, 4)
    u = d["u"].reshape(N, 128, 128, 4)
    x[:, :, :8] = 0
    u[:, :, ::16] = 0
    c, k = np.arange(C) // Z, np.arange(C) % Z
    o = rng.permutation(8)
    low = int(o[2])
    size = np.where(rng.permutation(N) < N // 2, 2.0 ** -30, 1.0)
    for r in range(N):
        m, n = rng.integers(E + 1, S - E, 2)
        at = int(rng.integers(E, S - E))
        one = 2 * int(rng.integers(E // 2, (S - E) // 2)) + 1
        even = c % 2 == 0
        side = c < m if r % 2 else c >= n
        h = r // 2 % 2 * (E - 2)
        cone = (k + np.abs(c - (S - 1 - h if r % 2 else h)) < E)
        more = rng.permutation(np.flatnonzero(cone & ~side))
        side[more[:int(np.sum(cone)) // 2 + 1 - int(np.sum(cone & side))]] = True
        kinds = [even, ~even, side, k + np.abs(c - at) < E, even | (c == one) & (k == 0)]
        rich = np.zeros((8, C), bool)
        rich[o[r % 2]] = True
        rich[low] = (k <= 2 * E) | (k == Z - 1)
        for g, i in zip(o[3:], rng.permutation(5)): rich[g] = kinds[i]
        small = np.where(np.arange(8) == low, 2.0 ** -30, size[r])
        mark = np.where(rich, 1, -rng.integers(0, 2, (8, C))) * small[:, None]
        for g in rng.permutation(np.delete(o, 2))[:4]:
            j = int(rng.integers(C))
            mark[g, j] = 2.0 ** 30 if rich[g, j] else -2.0 ** 30
        x[r, :, 0, :, 0] = mark
        x[r, low, 7, :, 0] = 2.0 ** -30
        for g in range(8): u[r, 16 * g, 16 * g, 0] = small[g]
        u[r, 16 * low + 1, 16 * low, 0] = 2.0 ** -30
    return {"x": x.reshape(N, 128, 4 * C).astype(BF), "u": u.reshape(N, 128, 512), "v": d["v"], **weights(rng, range(8), [low])}
def setup_inputs_huge(rng):
    d = numbers_of(rng)
    x = 2.0 ** 30 * (0.8 + 0.2 * rng.random((N, 128, C, 4)))
    c = np.stack([rng.permutation(C) % 2 * 2.0 - 1.0 for r in range(N)])
    c[rng.permutation(N) < N // 2] = 1
    x *= c[:, None, :, None]
    u = d["u"].reshape(N, 128, 8, 16, 4)
    s = np.stack([rng.permutation(8) % 2 * 2.0 - 1.0 for r in range(N)])
    a = 2.0 ** 30 * (1 - 0.1 * rng.random((N, 128, 8, 4))) * s[:, None, :, None]
    u[:, :, :, 0] = a.astype(np.float32).astype(BF)
    w = np.zeros((N, 128, 4, 128, 4), np.float32)
    i = np.arange(128)
    for b in range(4): w[:, i, b, i, b] = -1
    wc, ws = packed(w.reshape(N, 128, 2048).astype(BF), rng)
    return {"x": x.astype(np.float32).reshape(N, 128, 4 * C).astype(BF), "u": u.reshape(N, 128, 512), "v": d["v"], "wc": wc, "ws": ws}
def setup_inputs_spread(rng):
    d = setup_inputs(rng)
    d["x"] = big(wide(rng, N, 128, 4 * C, cols=6))
    return d
def check_inputs(d):
    b = []
    for k in ("x", "u", "v"):
        a = np.abs(d[k].astype(np.float32))
        if not (np.isfinite(a).all() and ((a == 0) | (a >= 2.0 ** -30) & (a <= 2.0 ** 30)).all()): b.append("a value of " + k)
    if ((d["wc"] & 0x7F) == 0x7F).any(): b.append("a code of wc that is no number")
    z = np.zeros((128, 4, 4), np.float32)
    z[:, 1] = 2.0 ** -30
    z[:, 2] = 2.0 ** 30
    c, s = emit(mx_ref.quantize(z.reshape(128, 16).astype(BF)))
    for r in range(N):
        p = mx_ref.live(d["ws"][r])
        if not ((p == s[0, 0]) | (p >= s[0, 1]) & (p <= s[0, 2])).all(): b.append("a scale of ws")
    return b
def reference(x, u, v, wc, ws):
    qu = [mx_ref.quantize(u[r]) for r in range(N)]
    lay = [pk(wc[r], ws[r]) for r in range(N)]
    now = [x[r] for r in range(N)]
    a = []
    for t in range(R):
        a, held, sent = [], [], []
        for r in range(N):
            q = mx_ref.quantize(now[r])
            a.append(cuts(mx_ref.matmul(qu[r], q)))
            held.append(decode(q).astype(BF))
            sent.append(mx_ref.quantize(gcols(held[r], slots(a[r]))))
        for r in range(N):
            s = (r - 1 - t) % N
            d = decode(sent[s])
            h = tile([mx_ref.matmul(pick(lay[r], np.arange(128 * b, 128 * b + 128)), sent[s]) * np.float32(0.015625) + d[:, b::4] for b in range(4)])
            now[r] = gcols(np.concatenate([held[r], h], axis=1), places(a[r], a[s]))
    y, oa = np.zeros((N, 128, C), np.float32), np.zeros((N, 8, S), np.float32)
    oc, osc = np.zeros((N, 128, 4 * C), np.uint8), np.zeros((N, 16, C), np.uint8)
    for r in range(N):
        q = mx_ref.quantize(now[r])
        y[r] = mx_ref.matmul(mx_ref.quantize(v[r]), q)
        oa[r] = a[r]
        oc[r], osc[r] = emit(q)
    return {"y": y, "oa": oa, "oc": oc, "osc": osc}

@@ -1,0 +1,431 @@
+from concourse.mybir import dt, AluOpType, ActivationFunctionType
+
+ALU = AluOpType
+ACT = ActivationFunctionType
+S, E, A, C, R = 20, 8, 160, 320, 3
+BF, F32, I32, U16, MXC, MXS = "bfloat16", "float32", "int32", "uint16", "float8_e4m3fn_x4", "uint8"
+SMALL = 0.015625
+CUT, CUT2 = 12, 8
+
+SCRATCH = {}
+
+
+def _sb(name, n, d):
+    SCRATCH[name] = ("sbuf", [128, n], d)
+
+
+def _mx(name, n):
+    _sb("q" + name, n, MXC)
+    _sb("s" + name, n, MXS)
+
+
+for _n, _w, _d in [("xin", 4 * C, BF), ("uin", 512, BF), ("vin", 512, BF), ("ft", 512, BF), ("ct", 4 * A, BF),
+                   ("zb", 516, BF), ("pi", 8, I32), ("pf", 16, F32), ("kv", 192, F32), ("a1", 192, BF), ("a2", 192, BF),
+                   ("m1", 192, BF), ("m2", 192, BF), ("m3", 192, BF), ("cc", 3 * S, F32), ("df", A, BF), ("db", S, BF),
+                   ("lp", 32, U16), ("ws0", 16 + 2 * A, BF), ("ws1", 16 + 2 * A, BF), ("yb0", A, F32), ("yb1", A, F32),
+                   ("oab", 2 * S, F32), ("lf", 2 * S, U16)]:
+    _sb(_n, _w, _d)
+for _n, _w in [("w", 512), ("u", 128), ("ur", 128), ("v", 128), ("xn", C), ("c", A), ("e", 512), ("x3", C)]:
+    _mx(_n, _w)
+for _t in range(R):
+    _mx("x%d" % _t, C)
+    _mx("l%d" % _t, A)
+    _mx("b%d" % _t, A)
+    _mx("f%d" % _t, 128)
+    for _n, _w, _d in [("xs", 4 * C, BF), ("bt", 4 * A, BF), ("wa", 6 * A, BF), ("wb", 6 * A, BF), ("val", A, BF),
+                       ("fw", A, BF), ("ow", 7 * S, F32), ("rx", 4 * S, F32), ("snd", 2 * S, U16), ("lnd", 2 * S, U16)]:
+        _sb(_n + str(_t), _w, _d)
+for _t in range(R - 1):
+    _sb("lt%d" % _t, S, U16)
+    _sb("lx%d" % _t, S, U16)
+for _b in range(8):
+    SCRATCH["ps%d" % _b] = ("psum", [128, 512], F32)
+
+SEMAPHORES = (["cV", "cA", "cP", "cG", "dx", "du", "dw", "dv", "stS", "stA", "gone"]
+              + ["rq%d" % t for t in range(R)] + ["rl%d" % t for t in range(R)])
+
+
+def _schedule(g, T, ops, arrivals, extra):
+    queue = {"V": g.vector, "A": g.scalar, "P": g.tensor, "G": g, "S": g.sync}
+    writer, readers, deps = dict(arrivals), {}, []
+    marked = set()
+    for i, (eng, fn, r, w, sem) in enumerate(ops):
+        d = []
+        for k in r:
+            d.append(writer[k])
+        for k in w:
+            if k in writer:
+                d.append(writer[k])
+            d.extend(readers.get(k, []))
+        d = [x for x in d if x != i]
+        deps.append(d)
+        for x in d:
+            if isinstance(x, int):
+                marked.add(x)
+        for k in r:
+            readers.setdefault(k, []).append(i)
+        for k in w:
+            writer[k] = i
+            readers[k] = []
+    total = dict(extra)
+    shared = {}
+    for eng, fn, r, w, sem in ops:
+        if sem is not None:
+            shared[sem] = shared.get(sem, 0) + 16
+    know = {e: {} for e in queue}
+    done, waited = {}, {}
+    for i, (eng, fn, r, w, sem) in enumerate(ops):
+        local = sorted(set(x for x in deps[i] if isinstance(x, int)), reverse=True)
+        need = [done[x] for x in local] + [(x[0], x[1], {}) for x in deps[i] if not isinstance(x, int)]
+        for s, v, kn in need:
+            if know[eng].get(s, 0) >= v:
+                continue
+            queue[eng].wait_ge(T.sem[s], v)
+            waited[s] = max(waited.get(s, 0), v)
+            know[eng][s] = v
+            for s2, v2 in kn.items():
+                know[eng][s2] = max(know[eng].get(s2, 0), v2)
+        ins = fn()
+        if sem is not None:
+            ins.then_inc(T.sem[sem], 16)
+            total[sem] = shared[sem]
+            done[i] = (sem, shared[sem], dict(know[eng]))
+        elif i in marked:
+            s = "c" + eng
+            total[s] = total.get(s, 0) + 1
+            ins.then_inc(T.sem[s], 1)
+            done[i] = (s, total[s], dict(know[eng]))
+    for s in sorted(total):
+        if waited.get(s, 0) < total[s]:
+            q = {"stS": g.sync, "stA": g.scalar}.get(s, g)
+            q.wait_ge(T.sem[s], total[s])
+
+
+def rank_program(g, core, T, topo):
+    rank = T.rank_of(core)
+    if rank is None:
+        return
+    n_ranks = len(T.cores)
+    V, SC, PE = g.vector, g.scalar, g.tensor
+    ops = []
+
+    def op(eng, fn, r, w, sem=None):
+        ops.append((eng, fn, r, w, sem))
+
+    common = set.intersection(*[set(topo.engines(a, b)) for a in T.cores for b in T.cores if a != b])
+    mask, ne = sum(1 << e for e in common), len(common)
+
+    arrivals, extra = {}, {"gone": 0}
+    for t in range(R):
+        arrivals["LQ%d" % t] = ("rq%d" % t, 2 * ne)
+        arrivals["LL%d" % t] = ("rl%d" % t, ne)
+        extra["rq%d" % t] = 2 * ne
+        extra["rl%d" % t] = ne
+
+    def send(t, out, in_, sem, r):
+        dst = T.cores[(rank + 1 + t) % n_ranks]
+        rid, pid = topo.addr(dst, core)
+        extra["gone"] += ne
+        op("G", lambda: g.remote_dma(out, in_, T.sem[sem], T.sem.gone, pid, rid, mask), r, [])
+
+    def ts(out, in0, s1, s2, o0, o1, r, w):
+        if o1 is None:
+            op("V", lambda: V.tensor_scalar(out, in0, s1, None, o0), r, w)
+        else:
+            op("V", lambda: V.tensor_scalar(out, in0, s1, s2, o0, o1), r, w)
+
+    def tt(out, a, b, o, r, w):
+        op("V", lambda: V.tensor_tensor(out, a, b, o), r, w)
+
+    def cp(out, in_, r, w):
+        op("V", lambda: V.tensor_copy(out, in_), r, w)
+
+    def fill(ap, c, w):
+        op("V", lambda: V.memset(ap, c), [], w)
+
+    def act(out, in_, func, r, w, **kw):
+        op("A", lambda: SC.activation(out, in_, func, **kw), r, w)
+
+    def quant(name, a, b, in_, r, w):
+        op("V", lambda: V.quantize_mx(T["q" + name][:, a:b], T["s" + name][:, a:b], in_), r, w)
+
+    def pick(dst, a, b, src, n, off, r, wq, wsc):
+        op("V", lambda: V.tensor_copy(T["q" + dst][:, a:b].bitcast(dt.uint32),
+                                      T["q" + src][:, 0:n].bitcast(dt.uint32).indirect(off)), r, [wq])
+        op("A", lambda: SC.activation(T["s" + dst][:, a:b], T["s" + src][:, 0:n].indirect(off), ACT.Copy), r, [wsc])
+
+    def mm(bank, terms, r):
+        def fn():
+            ins = None
+            for i, (ln, la, rn, ra, n) in enumerate(terms):
+                ins = PE.matmul_mx(T["ps%d" % bank][:, 0:n], T["q" + ln][:, la:la + 128], T["s" + ln][:, la:la + 128],
+                                   T["q" + rn][:, ra:ra + n], T["s" + rn][:, ra:ra + n], i == 0, i == len(terms) - 1)
+            return ins
+        op("P", fn, r, ["B%d" % bank])
+
+    def out_of(eng, bank, win, base, b, n, *keys):
+        dst = T[win[b & 1]][:, base + (b >> 1):base + 2 * n:2]
+        src = T["ps%d" % bank][:, 0:n]
+        w = ["B%d" % bank] + [k + str(b) for k in keys]
+        if eng == "V":
+            ts(dst, src, SMALL, None, ALU.mult, None, [], w)
+        else:
+            act(dst, src, ACT.Copy, [], w, scale=SMALL)
+
+    def gather(eng, o, out, win, n, off, r, keys, w):
+        src = T[win[o]][:, 0:n].indirect(off)
+        rr = r + [k + str(b) for k in keys for b in (o, o + 2)]
+        if eng == "V":
+            cp(out, src, rr, [w + str(o)])
+        else:
+            act(out, src, ACT.Copy, rr, [w + str(o)])
+
+    pf = lambda j: T.pf[:, j:j + 1]
+    P_, K2, Q_, Q8, CP, S1, S2, P2, P1, Q320, NK2 = range(11)
+    own = lambda t: ("wa%d" % t, "wb%d" % t)
+    snd = ("ws0", "ws1")
+
+    op("S", lambda: g.sync.dma_start(T.xin[:], T.x[:]), [], ["xin"], "dx")
+    op("S", lambda: g.sync.dma_start(T.uin[:], T.u[:]), [], ["uin"], "du")
+    op("S", lambda: g.sync.dma_start(T.qw[:].bitcast(dt.uint8), T.wc[:]), ["xin"], ["qw"], "dw")
+    op("S", lambda: g.sync.dma_start(T.sw[:], T.ws[:]), [], ["sw"], "dw")
+
+    flag = dict(allow_small_or_imprecise_dtypes=True)
+    op("G", lambda: g.iota(T.pi[:, 0:1], [[1, 1]], 0, 1), [], ["pi0"])
+    op("G", lambda: g.iota(T.kv[:], [[2, 192]], 0, 0, **flag), [], ["kv"])
+    op("G", lambda: g.iota(T.a1[:], [[-1, 24], [1, E]], 4, -1, **flag), [], ["a1"])
+    op("G", lambda: g.iota(T.a2[:], [[1, 24], [1, E]], -4, -1, **flag), [], ["a2"])
+    fill(T.ct[:], 0.0, ["ct0", "ct1"])
+    for j, (o, s) in enumerate([(ALU.bitwise_and, 14), (ALU.bitwise_and, 15), (ALU.bitwise_and, 8),
+                                (ALU.arith_shift_right, 3)]):
+        ts(T.pi[:, j + 1:j + 2], T.pi[:, 0:1], s, None, o, None, ["pi0"], ["pi%d" % (j + 1)])
+    fill(T.zb[:], 0.0, ["zb"])
+    cp(T.pf[:, 0:5], T.pi[:, 0:5], ["pi%d" % j for j in range(5)], ["pf"])
+    fill(T.ft[:], 0.0, ["ft0", "ft1"])
+    act(pf(S1), pf(CP), ACT.Copy, ["pf"], ["s1"], scale=-9.0)
+    act(pf(S2), pf(CP), ACT.Copy, ["pf"], ["s2"], scale=-7.0)
+    act(pf(P2), pf(P_), ACT.Copy, ["pf"], ["p2"], scale=2.0)
+    act(pf(P1), pf(K2), ACT.Identity, ["pf"], ["p1"], scale=-2.0, bias=pf(Q_))
+    act(pf(NK2), pf(K2), ACT.Copy, ["pf"], ["nk2"], scale=-1.0)
+    act(pf(Q320), pf(Q_), ACT.Identity, ["pf", "kv"], ["q320"], bias=T.kv[:, A:A + 1])
+    c0 = T.kv[:, 0:A:8]
+    cK, cN, cOwn = T.cc[:, 0:S], T.cc[:, S:2 * S], T.cc[:, 2 * S:3 * S]
+    act(cK, c0, ACT.Identity, ["kv", "pf"], ["cK"], bias=pf(K2))
+    act(cN, T.kv[:, 8:8 + A:8], ACT.Identity, ["kv", "nk2"], ["cN"], bias=pf(NK2))
+    act(cOwn, T.kv[:, 7:7 + A:8], ACT.Identity, ["kv", "p1"], ["cOwn"], bias=pf(P1))
+    cp(T.lp[:, 0:8], T.kv[:, 0:64:8], ["kv"], ["lu"])
+    ts(T.lp[:, 8:18], T.kv[:, 0:A:16], pf(Q_), pf(Q8), ALU.add, ALU.add, ["kv", "pf"], ["lpt"])
+    ts(T.lp[:, 18:28], T.kv[:, 4:4 + A:16], pf(Q_), pf(Q8), ALU.add, ALU.add, ["kv", "pf"], ["lpb"])
+    fill(T.df[:], 0.0, ["df"])
+    ts(T.zb[:, 3:515:4], T.kv[:, 0:128], pf(P2), 64.0, ALU.is_equal, ALU.mult, ["kv", "p2"], ["zb"])
+    fill(T.db[:], -18.0, ["db"])
+    fill(T.ws0[:, 0:16], 0.0, ["pad0", "pad2"])
+    fill(T.ws1[:, 0:16], 0.0, ["pad1", "pad3"])
+    fill(T.df[:, 8:A:8], 14.0, ["df"])
+    ts(T.m1[:], T.a1[:], pf(S1), 2048.0, ALU.is_ge, ALU.mult, ["a1", "s1"], ["m1"])
+    ts(T.m2[:], T.a2[:], pf(S2), None, ALU.is_ge, None, ["a2", "s2"], ["m2"])
+    quant("e", 0, 128, T.zb[:, 3:515], ["zb"], ["e0"])
+    tt(T.m3[:], T.m1[:], T.m2[:], ALU.mult, ["m1", "m2"], ["m3"])
+    act(T.ct[:, 0:4 * A:4], T.m3[:, 32:192], ACT.Copy, ["m3"], ["ct0"])
+    act(T.ct[96:128, 1:4 * A:4], T.m3[96:128, 0:A], ACT.Copy, ["m3"], ["ct1"])
+    quant("e", 128, 256, T.zb[:, 2:514], ["zb"], ["e1"])
+
+    top = lambda t: ["qt%d" % t, "st%d" % t]
+    bot = lambda t: ["qb%d" % t, "sb%d" % t]
+
+    def send_top(t):
+        send(t, T["ql%d" % t][:].bitcast(dt.uint8), T["qx%d" % t][:, 0:A].bitcast(dt.uint8), "rq%d" % t, top(t))
+        send(t, T["sl%d" % t][:], T["sx%d" % t][:, 0:A], "rq%d" % t, top(t))
+
+    def scores(t, b0, b1):
+        mm(b0, [("x%d" % t, 0, "ur", 0, 128)], top(t) + ["qur", "sur"])
+        mm(b1, [("x%d" % t, 32, "ur", 0, 128)], top(t) + ["qur", "sur"])
+
+    def signs(t, b0, b1):
+        ts(T.ft[:, 0:512:4], T["ps%d" % b0][:, 0:128], 0.0, 0.5, ALU.is_gt, ALU.subtract, [], ["B%d" % b0, "ft0"])
+        ts(T.ft[96:128, 1:512:4], T["ps%d" % b1][96:128, 0:128], 0.0, 0.5, ALU.is_gt, ALU.subtract, [],
+           ["B%d" % b1, "ft1"])
+        quant("f%d" % t, 0, 128, T.ft[:], ["ft0", "ft1"], ["qf%d" % t])
+
+    def cones(t, b):
+        mm(b, [("f%d" % t, 0, "c", 0, A)], ["qf%d" % t, "cone"])
+
+    ow = lambda t, j: T["ow%d" % t][:, S * j:S * j + S]
+    G_, M_, GP, Y_, N_, N2, A3 = range(7)
+
+    def cuts(t, b):
+        k = str(t)
+        val, fw, sl = T["val" + k], T["fw" + k], T["snd" + k]
+        tt(val[:], T["ps%d" % b][:, 0:A], T.kv[:, 1:1 + A], ALU.min, ["kv"], ["B%d" % b, "val" + k])
+        op("V", lambda: V.tensor_tensor_scan(fw[:], T.df[:], val[:], 0.0, ALU.add, ALU.max), ["df", "val" + k], ["fw" + k])
+        op("V", lambda: V.tensor_tensor_scan(T["ow" + k][:, S - 1::-1], T.db[:], fw[:, A - 1::-8], -1000.0,
+                                             ALU.add, ALU.max), ["db", "fw" + k], ["g" + k])
+        tt(ow(t, M_), ow(t, G_), cK, ALU.is_gt, ["g" + k, "cK"], ["m" + k])
+        tt(ow(t, GP), ow(t, G_), c0, ALU.max, ["g" + k, "kv"], ["gp" + k])
+        tt(ow(t, Y_), ow(t, M_), ow(t, G_), ALU.mult, ["m" + k, "g" + k], ["y" + k])
+        cp(sl[:, S:2 * S], ow(t, GP), ["gp" + k], ["sg" + k])
+        ts(sl[:, 0:S], ow(t, Y_), pf(P1), 14.0, ALU.add, ALU.add, ["y" + k, "p1"], ["sl" + k])
+        send(t, T["lnd" + k][:], sl[:], "rl" + k, ["sg" + k, "sl" + k])
+
+    lt = lambda t: T["lt%d" % t][:] if t < R - 1 else T.lf[:, 0:2 * S:2]
+    lx = lambda t: T["lx%d" % t][:] if t < R - 1 else T.lf[:, 1:2 * S:2]
+
+    def own_list(t, j):
+        k = str(t)
+        if j == 0:
+            tt(ow(t, N_), ow(t, G_), cN, ALU.is_ge, ["g" + k, "cN"], ["n" + k])
+        elif j == 1:
+            ts(ow(t, N2), ow(t, N_), float(2 * A - 16), pf(Q320), ALU.mult, ALU.add, ["n" + k, "q320"], ["n2" + k])
+        elif j == 2:
+            tt(ow(t, A3), ow(t, GP), ow(t, N2), ALU.add, ["gp" + k, "n2" + k], ["a3" + k])
+        else:
+            ts(lt(t), ow(t, A3), float(-2 * A), None, ALU.add, None, ["a3" + k], ["lt" + k])
+
+    def refill_list(t, j):
+        k = str(t)
+        rx = lambda i: T["rx" + k][:, S * i:S * i + S]
+        if j == 0:
+            ts(rx(0), T["lnd" + k][:, S:2 * S], pf(K2), 16.0, ALU.subtract, ALU.add, ["LL" + k, "pf"], ["r0" + k])
+        elif j == 1:
+            tt(rx(1), rx(0), ow(t, GP), ALU.is_gt, ["r0" + k, "gp" + k], ["r1" + k])
+        elif j == 2:
+            tt(rx(2), rx(1), ow(t, A3), ALU.mult, ["r1" + k, "a3" + k], ["r2" + k])
+        elif j == 3:
+            tt(rx(3), rx(2), cOwn, ALU.max, ["r2" + k, "cOwn"], ["r3" + k])
+        else:
+            cp(lx(t), rx(3), ["r3" + k], ["lx" + k])
+
+    def unpack(bank, b, name, a, n, r):
+        mm(bank, [("e", 128 * b, name, a, n)], r + ["e%d" % b])
+
+    def slots(eng, t, o):
+        gather(eng, o, T["bt%d" % t][:, o:4 * A:2], snd, 16 + 2 * A, T["lnd%d" % t][:, 0:S], ["LL%d" % t],
+               ["pad", "ts"], "bt%d" % t)
+
+    eng_of = lambda b: "A" if b & 1 else "V"
+    order = (1, 0, 3, 2)
+    late = (1, 3, 0, 2)
+
+    def refill(t, bank):
+        refill_list(t, 0)
+        quant("b%d" % t, 0, A, T["bt%d" % t][:], ["bt%d0" % t, "bt%d1" % t], ["qB%d" % t])
+        for b in late:
+            mm(bank[b], [("w", 128 * b, "b%d" % t, 0, A), ("e", 128 * b, "b%d" % t, 0, A)],
+               ["qB%d" % t, "qw", "sw", "e%d" % b])
+        for j in range(4):
+            refill_list(t, j + 1)
+            if t + 1 < R:
+                own_list(t + 1, j)
+        for b in late:
+            out_of(eng_of(b), bank[b], own(t), 4 * A, b, A, "h%d" % t)
+
+    def new_top(t):
+        for eng, o in (("A", 1), ("V", 0)):
+            gather(eng, o, T["xs%d" % t][:, o:4 * A:2], own(t), 4 * A, lt(t), ["lt%d" % t],
+                   ["tt%d" % t, "tb%d" % t], "xt%d" % t)
+        quant("x%d" % (t + 1), 0, A, T["xs%d" % t][:, 0:4 * A], ["xt%d0" % t, "xt%d1" % t], top(t + 1))
+
+    def new_bottom(t):
+        for eng, o, a, b in (("A", 1, 0, S), ("V", 0, 0, CUT), ("A", 0, CUT, S)):
+            gather(eng, o, T["xs%d" % t][:, 4 * A + 32 * a + o:4 * A + 32 * b:2], own(t), 6 * A, T["lx%d" % t][:, a:b],
+                   ["lx%d" % t], ["tt%d" % t, "tb%d" % t, "h%d" % t], "xb%d%s" % (t, eng))
+        quant("x%d" % (t + 1), A, C, T["xs%d" % t][:, 4 * A:8 * A], ["xb%dA0" % t, "xb%dA1" % t, "xb%dV0" % t],
+              bot(t + 1))
+
+    quant("xn", 0, C, T.xin[:], ["xin"], ["qxn"])
+    pick("x0", 0, A, "xn", C, T.lp[:, 8:18], ["qxn", "lpt"], "qt0", "st0")
+    send_top(0)
+    quant("c", 0, A, T.ct[:], ["ct0", "ct1"], ["cone"])
+    quant("u", 0, 128, T.uin[:], ["uin"], ["qu"])
+    quant("e", 256, 384, T.zb[:, 1:513], ["zb"], ["e2"])
+    pick("ur", 0, 128, "u", 128, T.lp[:, 0:8], ["qu", "lu"], "qur", "sur")
+    scores(0, 4, 5)
+    pick("x0", A, C, "xn", C, T.lp[:, 18:28], ["qxn", "lpb"], "qb0", "sb0")
+    signs(0, 4, 5)
+    for b in range(4):
+        if b == 2:
+            cones(0, 4)
+            quant("e", 384, 512, T.zb[:, 0:512], ["zb"], ["e3"])
+        unpack(b, b, "x0", 0, C, top(0) + bot(0))
+        out_of("A", b, own(0), 0, b, C, "tt0", "tb0")
+    cuts(0, 4)
+    for j in range(4):
+        own_list(0, j)
+    new_top(0)
+    send_top(1)
+    op("S", lambda: g.sync.dma_start(T.vin[:], T.v[:]), top(1), ["vin"], "dv")
+    scores(1, 4, 5)
+    for b in range(4):
+        if b == 2:
+            signs(1, 4, 5)
+            cones(1, 4)
+        unpack(b, b, "x1", 0, A, top(1))
+        out_of("A", b, own(1), 0, b, A, "tt1")
+    bank = {1: 6, 0: 7, 3: 0, 2: 1}
+    for b in order:
+        unpack(bank[b], b, "l0", 0, A, ["LQ0"])
+    cuts(1, 4)
+    for b in order:
+        out_of(eng_of(b), bank[b], snd, 16, b, A, "ts")
+    slots("A", 0, 1)
+    slots("V", 0, 0)
+    refill(0, {1: 2, 3: 3, 0: 4, 2: 5})
+    new_bottom(0)
+    for b in order:
+        unpack(b, b, "x1", A, A, bot(1))
+        out_of(eng_of(b), b, own(1), 2 * A, b, A, "tb1")
+    for b in range(4):
+        unpack(4 + b, b, "l1", 0, A, ["LQ1"])
+    new_top(1)
+    send_top(2)
+    scores(2, 0, 1)
+    for b in range(4):
+        out_of("A", 4 + b, snd, 16, b, A, "ts")
+    signs(2, 0, 1)
+    cones(2, 2)
+    quant("v", 0, 128, T.vin[:], ["vin"], ["qv"])
+    slots("A", 1, 0)
+    slots("A", 1, 1)
+    bank = {0: 0, 1: 1, 2: 3, 3: 4}
+    for b in range(4):
+        unpack(bank[b], b, "x2", 0, A, top(2))
+        out_of("A", bank[b], own(2), 0, b, A, "tt2")
+    cuts(2, 2)
+    refill(1, {1: 5, 3: 6, 0: 7, 2: 2})
+    new_bottom(1)
+    low = {0: 5, 1: 6, 2: 7, 3: 2}
+    for b in range(4):
+        unpack(low[b], b, "x2", A, A, bot(2))
+    bank = {1: 0, 0: 1, 3: 3, 2: 4}
+    for b in order:
+        unpack(bank[b], b, "l2", 0, A, ["LQ2"])
+    tt(T.oab[:, 0:S], ow(2, GP), c0, ALU.subtract, ["gp2", "kv"], ["oa0"])
+    ts(T.oab[:, S:2 * S], T.oab[:, 0:S], 0.5, None, ALU.mult, None, ["oa0"], ["oa1"])
+    op("S", lambda: g.sync.dma_start(T.oa[:], T.oab[0:128:16, S:2 * S]), ["oa1"], [], "stS")
+    for b in order:
+        out_of(eng_of(b), bank[b], snd, 16, b, A, "ts")
+    slots("A", 2, 1)
+    slots("V", 2, 0)
+    for b in late:
+        out_of("A", low[b], own(2), 2 * A, b, A, "tb2")
+    refill(2, {1: 0, 3: 1, 0: 3, 2: 4})
+    for h in range(2):
+        parts = (("A", 1, 0, S), ("V", 0, 0, S)) if h == 0 else (("A", 1, 0, S), ("V", 0, 0, CUT2), ("A", 0, CUT2, S))
+        for eng, o, a, b in parts:
+            gather(eng, o, T.xs2[:, 4 * A * h + 32 * a + o:4 * A * h + 32 * b:2], own(2), 6 * A,
+                   T.lf[:, S * h + a:S * h + b], ["lt2", "lx2"], ["tt2", "tb2", "h2"], "x3%d%s" % (h, eng))
+        quant("x3", A * h, A * h + A, T.xs2[:, 4 * A * h:4 * A * (h + 1)],
+              ["x3%d%s%d" % (h, eng, o) for eng, o, a, b in parts], ["q3%d" % h])
+        mm(5 + h, [("v", 0, "x3", A * h, A)], ["qv", "q3%d" % h])
+        op("S", lambda h=h: g.sync.dma_start(T.oc[:, 4 * A * h:4 * A * (h + 1)],
+                                             T.qx3[:, A * h:A * h + A].bitcast(dt.uint8)), ["q3%d" % h], [], "stS")
+    act(T.yb0[:], T.ps5[:, 0:A], ACT.Copy, [], ["B5", "yb0"])
+    op("A", lambda: SC.dma_start(T.y[:, 0:A], T.yb0[:]), ["yb0"], [], "stA")
+    cp(T.yb1[:], T.ps6[:, 0:A], [], ["B6", "yb1"])
+    for k in range(2):
+        op("A", lambda k=k: SC.dma_start(T.osc[4 * k:4 * k + 4, :], T.sx3[32 * k:32 * k + 4, :]), ["q30", "q31"], [], "stA")
+    for k in range(2, 4):
+        op("S", lambda k=k: g.sync.dma_start(T.osc[4 * k:4 * k + 4, :], T.sx3[32 * k:32 * k + 4, :]), ["q30", "q31"], [], "stS")
+    op("A", lambda: SC.dma_start(T.y[:, A:C], T.yb1[:]), ["yb1"], [], "stA")
+
+    _schedule(g, T, ops, arrivals, extra)

@@ -22,7 +22,7 @@ def _mx(name, n):
 for _n, _w, _d in [("xin", 4 * C, BF), ("uin", 512, BF), ("vin", 512, BF), ("ft", 512, BF), ("ct", 4 * A, BF),
                    ("zb", 516, BF), ("pi", 8, I32), ("pf", 16, F32), ("kv", 192, F32), ("a1", 192, BF), ("a2", 192, BF),
                    ("m1", 192, BF), ("m2", 192, BF), ("m3", 192, BF), ("cc", 3 * S, F32), ("df", A, BF), ("db", S, BF),
-                   ("lp", 32, U16), ("ws0", 16 + 2 * A, BF), ("ws1", 16 + 2 * A, BF), ("yb0", A, F32), ("yb1", A, F32),
+                   ("lp", 32, U16), ("ws0", 16 + 2 * A, BF), ("ws1", 16 + 2 * A, BF), ("yb", C, F32),
                    ("oab", 2 * S, F32), ("lf", 2 * S, U16)]:
     _sb(_n, _w, _d)
 for _n, _w in [("w", 512), ("u", 128), ("ur", 128), ("v", 128), ("xn", C), ("c", A), ("e", 512), ("x3", C)]:
@@ -195,16 +195,17 @@ def rank_program(g, core, T, topo):
     op("G", lambda: g.iota(T.kv[:], [[2, 192]], 0, 0, **flag), [], ["kv"])
     op("G", lambda: g.iota(T.a1[:], [[-1, 24], [1, E]], 4, -1, **flag), [], ["a1"])
     op("G", lambda: g.iota(T.a2[:], [[1, 24], [1, E]], -4, -1, **flag), [], ["a2"])
+    op("G", lambda: g.iota(T.ft[:], [[0, 512]], 0, 0, **flag), [], ["ft0", "ft1"])
     fill(T.ct[:], 0.0, ["ct0", "ct1"])
     for j, (o, s) in enumerate([(ALU.bitwise_and, 14), (ALU.bitwise_and, 15), (ALU.bitwise_and, 8),
                                 (ALU.arith_shift_right, 3)]):
         ts(T.pi[:, j + 1:j + 2], T.pi[:, 0:1], s, None, o, None, ["pi0"], ["pi%d" % (j + 1)])
     fill(T.zb[:], 0.0, ["zb"])
     cp(T.pf[:, 0:5], T.pi[:, 0:5], ["pi%d" % j for j in range(5)], ["pf"])
-    fill(T.ft[:], 0.0, ["ft0", "ft1"])
+    fill(T.df[:], 0.0, ["df"])
+    act(pf(P2), pf(P_), ACT.Copy, ["pf"], ["p2"], scale=2.0)
     act(pf(S1), pf(CP), ACT.Copy, ["pf"], ["s1"], scale=-9.0)
     act(pf(S2), pf(CP), ACT.Copy, ["pf"], ["s2"], scale=-7.0)
-    act(pf(P2), pf(P_), ACT.Copy, ["pf"], ["p2"], scale=2.0)
     act(pf(P1), pf(K2), ACT.Identity, ["pf"], ["p1"], scale=-2.0, bias=pf(Q_))
     act(pf(NK2), pf(K2), ACT.Copy, ["pf"], ["nk2"], scale=-1.0)
     act(pf(Q320), pf(Q_), ACT.Identity, ["pf", "kv"], ["q320"], bias=T.kv[:, A:A + 1])
@@ -216,19 +217,19 @@ def rank_program(g, core, T, topo):
     cp(T.lp[:, 0:8], T.kv[:, 0:64:8], ["kv"], ["lu"])
     ts(T.lp[:, 8:18], T.kv[:, 0:A:16], pf(Q_), pf(Q8), ALU.add, ALU.add, ["kv", "pf"], ["lpt"])
     ts(T.lp[:, 18:28], T.kv[:, 4:4 + A:16], pf(Q_), pf(Q8), ALU.add, ALU.add, ["kv", "pf"], ["lpb"])
-    fill(T.df[:], 0.0, ["df"])
     ts(T.zb[:, 3:515:4], T.kv[:, 0:128], pf(P2), 64.0, ALU.is_equal, ALU.mult, ["kv", "p2"], ["zb"])
     fill(T.db[:], -18.0, ["db"])
     fill(T.ws0[:, 0:16], 0.0, ["pad0", "pad2"])
     fill(T.ws1[:, 0:16], 0.0, ["pad1", "pad3"])
     fill(T.df[:, 8:A:8], 14.0, ["df"])
+    quant("e", 0, 128, T.zb[:, 3:515], ["zb"], ["e0"])
     ts(T.m1[:], T.a1[:], pf(S1), 2048.0, ALU.is_ge, ALU.mult, ["a1", "s1"], ["m1"])
     ts(T.m2[:], T.a2[:], pf(S2), None, ALU.is_ge, None, ["a2", "s2"], ["m2"])
-    quant("e", 0, 128, T.zb[:, 3:515], ["zb"], ["e0"])
+    quant("e", 128, 256, T.zb[:, 2:514], ["zb"], ["e1"])
     tt(T.m3[:], T.m1[:], T.m2[:], ALU.mult, ["m1", "m2"], ["m3"])
     act(T.ct[:, 0:4 * A:4], T.m3[:, 32:192], ACT.Copy, ["m3"], ["ct0"])
     act(T.ct[96:128, 1:4 * A:4], T.m3[96:128, 0:A], ACT.Copy, ["m3"], ["ct1"])
-    quant("e", 128, 256, T.zb[:, 2:514], ["zb"], ["e1"])
+    quant("e", 256, 384, T.zb[:, 1:513], ["zb"], ["e2"])
 
     top = lambda t: ["qt%d" % t, "st%d" % t]
     bot = lambda t: ["qb%d" % t, "sb%d" % t]
@@ -255,17 +256,26 @@ def rank_program(g, core, T, topo):
 
     def cuts(t, b):
         k = str(t)
-        val, fw, sl = T["val" + k], T["fw" + k], T["snd" + k]
+        val, fw = T["val" + k], T["fw" + k]
         tt(val[:], T["ps%d" % b][:, 0:A], T.kv[:, 1:1 + A], ALU.min, ["kv"], ["B%d" % b, "val" + k])
         op("V", lambda: V.tensor_tensor_scan(fw[:], T.df[:], val[:], 0.0, ALU.add, ALU.max), ["df", "val" + k], ["fw" + k])
         op("V", lambda: V.tensor_tensor_scan(T["ow" + k][:, S - 1::-1], T.db[:], fw[:, A - 1::-8], -1000.0,
                                              ALU.add, ALU.max), ["db", "fw" + k], ["g" + k])
-        tt(ow(t, M_), ow(t, G_), cK, ALU.is_gt, ["g" + k, "cK"], ["m" + k])
-        tt(ow(t, GP), ow(t, G_), c0, ALU.max, ["g" + k, "kv"], ["gp" + k])
-        tt(ow(t, Y_), ow(t, M_), ow(t, G_), ALU.mult, ["m" + k, "g" + k], ["y" + k])
-        cp(sl[:, S:2 * S], ow(t, GP), ["gp" + k], ["sg" + k])
-        ts(sl[:, 0:S], ow(t, Y_), pf(P1), 14.0, ALU.add, ALU.add, ["y" + k, "p1"], ["sl" + k])
-        send(t, T["lnd" + k][:], sl[:], "rl" + k, ["sg" + k, "sl" + k])
+
+    def slot_list(t, j):
+        k = str(t)
+        sl = T["snd" + k]
+        if j == 0:
+            tt(ow(t, M_), ow(t, G_), cK, ALU.is_gt, ["g" + k, "cK"], ["m" + k])
+        elif j == 1:
+            tt(ow(t, GP), ow(t, G_), c0, ALU.max, ["g" + k, "kv"], ["gp" + k])
+        elif j == 2:
+            tt(ow(t, Y_), ow(t, M_), ow(t, G_), ALU.mult, ["m" + k, "g" + k], ["y" + k])
+        elif j == 3:
+            cp(sl[:, S:2 * S], ow(t, GP), ["gp" + k], ["sg" + k])
+        else:
+            ts(sl[:, 0:S], ow(t, Y_), pf(P1), 14.0, ALU.add, ALU.add, ["y" + k, "p1"], ["sl" + k])
+            send(t, T["lnd" + k][:], sl[:], "rl" + k, ["sg" + k, "sl" + k])
 
     lt = lambda t: T["lt%d" % t][:] if t < R - 1 else T.lf[:, 0:2 * S:2]
     lx = lambda t: T["lx%d" % t][:] if t < R - 1 else T.lf[:, 1:2 * S:2]
@@ -314,8 +324,14 @@ def rank_program(g, core, T, topo):
                ["qB%d" % t, "qw", "sw", "e%d" % b])
         for j in range(4):
             refill_list(t, j + 1)
-            if t + 1 < R:
-                own_list(t + 1, j)
+            if t == 0:
+                slot_list(1, j)
+            elif t == 1:
+                own_list(2, j)
+            elif j == 0:
+                quant("v", 0, 128, T.vin[:], ["vin"], ["qv"])
+        if t == 0:
+            slot_list(1, 4)
         for b in late:
             out_of(eng_of(b), bank[b], own(t), 4 * A, b, A, "h%d" % t)
 
@@ -329,6 +345,9 @@ def rank_program(g, core, T, topo):
         for eng, o, a, b in (("A", 1, 0, S), ("V", 0, 0, CUT), ("A", 0, CUT, S)):
             gather(eng, o, T["xs%d" % t][:, 4 * A + 32 * a + o:4 * A + 32 * b:2], own(t), 6 * A, T["lx%d" % t][:, a:b],
                    ["lx%d" % t], ["tt%d" % t, "tb%d" % t, "h%d" % t], "xb%d%s" % (t, eng))
+        if t == 0:
+            own_list(1, 0)
+            own_list(1, 1)
         quant("x%d" % (t + 1), A, C, T["xs%d" % t][:, 4 * A:8 * A], ["xb%dA0" % t, "xb%dA1" % t, "xb%dV0" % t],
               bot(t + 1))
 
@@ -337,7 +356,6 @@ def rank_program(g, core, T, topo):
     send_top(0)
     quant("c", 0, A, T.ct[:], ["ct0", "ct1"], ["cone"])
     quant("u", 0, 128, T.uin[:], ["uin"], ["qu"])
-    quant("e", 256, 384, T.zb[:, 1:513], ["zb"], ["e2"])
     pick("ur", 0, 128, "u", 128, T.lp[:, 0:8], ["qu", "lu"], "qur", "sur")
     scores(0, 4, 5)
     pick("x0", A, C, "xn", C, T.lp[:, 18:28], ["qxn", "lpb"], "qb0", "sb0")
@@ -349,11 +367,11 @@ def rank_program(g, core, T, topo):
         unpack(b, b, "x0", 0, C, top(0) + bot(0))
         out_of("A", b, own(0), 0, b, C, "tt0", "tb0")
     cuts(0, 4)
-    for j in range(4):
-        own_list(0, j)
+    for f, j in ((own_list, 0), (slot_list, 0), (slot_list, 1), (own_list, 1), (slot_list, 2), (slot_list, 3),
+                 (own_list, 2), (slot_list, 4), (own_list, 3)):
+        f(0, j)
     new_top(0)
     send_top(1)
-    op("S", lambda: g.sync.dma_start(T.vin[:], T.v[:]), top(1), ["vin"], "dv")
     scores(1, 4, 5)
     for b in range(4):
         if b == 2:
@@ -371,8 +389,12 @@ def rank_program(g, core, T, topo):
     slots("V", 0, 0)
     refill(0, {1: 2, 3: 3, 0: 4, 2: 5})
     new_bottom(0)
+    op("S", lambda: g.sync.dma_start(T.vin[:], T.v[:]), bot(1), ["vin"], "dv")
     for b in order:
         unpack(b, b, "x1", A, A, bot(1))
+    own_list(1, 2)
+    own_list(1, 3)
+    for b in order:
         out_of(eng_of(b), b, own(1), 2 * A, b, A, "tb1")
     for b in range(4):
         unpack(4 + b, b, "l1", 0, A, ["LQ1"])
@@ -383,7 +405,6 @@ def rank_program(g, core, T, topo):
         out_of("A", 4 + b, snd, 16, b, A, "ts")
     signs(2, 0, 1)
     cones(2, 2)
-    quant("v", 0, 128, T.vin[:], ["vin"], ["qv"])
     slots("A", 1, 0)
     slots("A", 1, 1)
     bank = {0: 0, 1: 1, 2: 3, 3: 4}
@@ -391,17 +412,17 @@ def rank_program(g, core, T, topo):
         unpack(bank[b], b, "x2", 0, A, top(2))
         out_of("A", bank[b], own(2), 0, b, A, "tt2")
     cuts(2, 2)
+    for j in range(5):
+        slot_list(2, j)
     refill(1, {1: 5, 3: 6, 0: 7, 2: 2})
-    new_bottom(1)
-    low = {0: 5, 1: 6, 2: 7, 3: 2}
-    for b in range(4):
-        unpack(low[b], b, "x2", A, A, bot(2))
     bank = {1: 0, 0: 1, 3: 3, 2: 4}
     for b in order:
         unpack(bank[b], b, "l2", 0, A, ["LQ2"])
+    new_bottom(1)
+    low = {0: 5, 1: 6, 2: 7, 3: 2}
+    for b in late:
+        unpack(low[b], b, "x2", A, A, bot(2))
     tt(T.oab[:, 0:S], ow(2, GP), c0, ALU.subtract, ["gp2", "kv"], ["oa0"])
-    ts(T.oab[:, S:2 * S], T.oab[:, 0:S], 0.5, None, ALU.mult, None, ["oa0"], ["oa1"])
-    op("S", lambda: g.sync.dma_start(T.oa[:], T.oab[0:128:16, S:2 * S]), ["oa1"], [], "stS")
     for b in order:
         out_of(eng_of(b), bank[b], snd, 16, b, A, "ts")
     slots("A", 2, 1)
@@ -414,18 +435,18 @@ def rank_program(g, core, T, topo):
         for eng, o, a, b in parts:
             gather(eng, o, T.xs2[:, 4 * A * h + 32 * a + o:4 * A * h + 32 * b:2], own(2), 6 * A,
                    T.lf[:, S * h + a:S * h + b], ["lt2", "lx2"], ["tt2", "tb2", "h2"], "x3%d%s" % (h, eng))
+        if h == 0:
+            ts(T.oab[:, S:2 * S], T.oab[:, 0:S], 0.5, None, ALU.mult, None, ["oa0"], ["oa1"])
+            op("S", lambda: g.sync.dma_start(T.oa[:], T.oab[0:128:16, S:2 * S]), ["oa1"], [], "stS")
         quant("x3", A * h, A * h + A, T.xs2[:, 4 * A * h:4 * A * (h + 1)],
               ["x3%d%s%d" % (h, eng, o) for eng, o, a, b in parts], ["q3%d" % h])
         mm(5 + h, [("v", 0, "x3", A * h, A)], ["qv", "q3%d" % h])
         op("S", lambda h=h: g.sync.dma_start(T.oc[:, 4 * A * h:4 * A * (h + 1)],
                                              T.qx3[:, A * h:A * h + A].bitcast(dt.uint8)), ["q3%d" % h], [], "stS")
-    act(T.yb0[:], T.ps5[:, 0:A], ACT.Copy, [], ["B5", "yb0"])
-    op("A", lambda: SC.dma_start(T.y[:, 0:A], T.yb0[:]), ["yb0"], [], "stA")
-    cp(T.yb1[:], T.ps6[:, 0:A], [], ["B6", "yb1"])
-    for k in range(2):
-        op("A", lambda k=k: SC.dma_start(T.osc[4 * k:4 * k + 4, :], T.sx3[32 * k:32 * k + 4, :]), ["q30", "q31"], [], "stA")
-    for k in range(2, 4):
+    act(T.yb[:, 0:A], T.ps5[:, 0:A], ACT.Copy, [], ["B5", "yb0"])
+    act(T.yb[:, A:C], T.ps6[:, 0:A], ACT.Copy, [], ["B6", "yb1"])
+    op("A", lambda: SC.dma_start(T.y[:], T.yb[:]), ["yb0", "yb1"], [], "stA")
+    for k in range(4):
         op("S", lambda k=k: g.sync.dma_start(T.osc[4 * k:4 * k + 4, :], T.sx3[32 * k:32 * k + 4, :]), ["q30", "q31"], [], "stS")
-    op("A", lambda: SC.dma_start(T.y[:, A:C], T.yb1[:]), ["yb1"], [], "stA")
 
     _schedule(g, T, ops, arrivals, extra)

@@ -7,6 +7,19 @@ BF, F32, I32, U16, MXC, MXS = "bfloat16", "float32", "int32", "uint16", "float8_
 SMALL = 0.015625
 CUT, CUT2 = 12, 8
 
+SWAP = (95, 112, 135, 136, 137, 138, 139, 150, 153, 208, 209, 216, 226)
+ORDER = (33, 16, 4, 12, 10, 30, 11, 36, 13, 5, 14, 15, 9, 0, 17, 34, 19, 6, 18, 7, 8, 29, 39, 26, 38, 40, 41, 1, 42, 27,
+         43, 21, 46, 28, 47, 48, 44, 52, 37, 23, 54, 49, 22, 20, 53, 55, 24, 57, 59, 56, 60, 51, 58, 61, 62, 25, 66, 67,
+         70, 45, 63, 71, 72, 73, 74, 75, 64, 77, 78, 80, 76, 68, 81, 79, 50, 65, 84, 69, 82, 86, 85, 87, 94, 32, 92, 31,
+         90, 95, 96, 91, 105, 93, 104, 107, 97, 3, 2, 114, 83, 112, 88, 98, 117, 111, 106, 99, 116, 113, 108, 115, 100,
+         102, 101, 118, 123, 109, 103, 125, 110, 127, 119, 89, 124, 120, 140, 126, 128, 121, 129, 122, 133, 130, 134,
+         131, 156, 157, 135, 136, 137, 155, 154, 138, 139, 166, 141, 142, 35, 144, 132, 147, 146, 168, 148, 165, 167,
+         153, 150, 149, 152, 145, 151, 159, 158, 160, 164, 163, 192, 170, 174, 181, 169, 179, 171, 175, 173, 172, 198,
+         193, 177, 183, 182, 195, 176, 200, 197, 184, 178, 196, 194, 207, 202, 185, 208, 204, 186, 162, 187, 161, 188,
+         143, 210, 211, 209, 189, 190, 199, 206, 180, 222, 214, 212, 215, 213, 201, 191, 216, 203, 223, 224, 205, 226,
+         225, 217, 228, 219, 221, 227, 234, 220, 233, 218, 239, 231, 235, 241, 230, 236, 232, 240, 229, 244, 242, 243,
+         237, 238, 246, 247, 245, 250, 248, 251, 249, 252, 257, 253, 255, 254, 261, 256, 258, 260, 259, 265, 264, 266,
+         262, 267, 263)
 SCRATCH = {}
 
 
@@ -22,8 +35,7 @@ def _mx(name, n):
 for _n, _w, _d in [("xin", 4 * C, BF), ("uin", 512, BF), ("vin", 512, BF), ("ft", 512, BF), ("ct", 4 * A, BF),
                    ("zb", 516, BF), ("pi", 8, I32), ("pf", 16, F32), ("kv", 192, F32), ("a1", 192, BF), ("a2", 192, BF),
                    ("m1", 192, BF), ("m2", 192, BF), ("m3", 192, BF), ("cc", 3 * S, F32), ("df", A, BF), ("db", S, BF),
-                   ("lp", 32, U16), ("ws0", 16 + 2 * A, BF), ("ws1", 16 + 2 * A, BF), ("yb", C, F32),
-                   ("oab", 2 * S, F32), ("lf", 2 * S, U16)]:
+                   ("lp", 32, U16), ("yb", C, F32), ("oab", 2 * S, F32), ("lf", 2 * S, U16)]:
     _sb(_n, _w, _d)
 for _n, _w in [("w", 512), ("u", 128), ("ur", 128), ("v", 128), ("xn", C), ("c", A), ("e", 512), ("x3", C)]:
     _mx(_n, _w)
@@ -33,6 +45,7 @@ for _t in range(R):
     _mx("b%d" % _t, A)
     _mx("f%d" % _t, 128)
     for _n, _w, _d in [("xs", 4 * C, BF), ("bt", 4 * A, BF), ("wa", 6 * A, BF), ("wb", 6 * A, BF), ("val", A, BF),
+                       ("pa", 16 + 2 * A, BF), ("pb", 16 + 2 * A, BF),
                        ("fw", A, BF), ("ow", 7 * S, F32), ("rx", 4 * S, F32), ("snd", 2 * S, U16), ("lnd", 2 * S, U16)]:
         _sb(_n + str(_t), _w, _d)
 for _t in range(R - 1):
@@ -128,6 +141,9 @@ def rank_program(g, core, T, topo):
         extra["gone"] += ne
         op("G", lambda: g.remote_dma(out, in_, T.sem[sem], T.sem.gone, pid, rid, mask), r, [])
 
+    def other(eng):
+        return {"V": "A", "A": "V"}[eng] if len(ops) in SWAP else eng
+
     def ts(out, in0, s1, s2, o0, o1, r, w):
         if o1 is None:
             op("V", lambda: V.tensor_scalar(out, in0, s1, None, o0), r, w)
@@ -167,6 +183,7 @@ def rank_program(g, core, T, topo):
         dst = T[win[b & 1]][:, base + (b >> 1):base + 2 * n:2]
         src = T["ps%d" % bank][:, 0:n]
         w = ["B%d" % bank] + [k + str(b) for k in keys]
+        eng = other(eng)
         if eng == "V":
             ts(dst, src, SMALL, None, ALU.mult, None, [], w)
         else:
@@ -175,6 +192,7 @@ def rank_program(g, core, T, topo):
     def gather(eng, o, out, win, n, off, r, keys, w):
         src = T[win[o]][:, 0:n].indirect(off)
         rr = r + [k + str(b) for k in keys for b in (o, o + 2)]
+        eng = other(eng)
         if eng == "V":
             cp(out, src, rr, [w + str(o)])
         else:
@@ -183,7 +201,7 @@ def rank_program(g, core, T, topo):
     pf = lambda j: T.pf[:, j:j + 1]
     P_, K2, Q_, Q8, CP, S1, S2, P2, P1, Q320, NK2 = range(11)
     own = lambda t: ("wa%d" % t, "wb%d" % t)
-    snd = ("ws0", "ws1")
+    snd = lambda t: ("pa%d" % t, "pb%d" % t)
 
     op("S", lambda: g.sync.dma_start(T.xin[:], T.x[:]), [], ["xin"], "dx")
     op("S", lambda: g.sync.dma_start(T.uin[:], T.u[:]), [], ["uin"], "du")
@@ -219,8 +237,9 @@ def rank_program(g, core, T, topo):
     ts(T.lp[:, 18:28], T.kv[:, 4:4 + A:16], pf(Q_), pf(Q8), ALU.add, ALU.add, ["kv", "pf"], ["lpb"])
     ts(T.zb[:, 3:515:4], T.kv[:, 0:128], pf(P2), 64.0, ALU.is_equal, ALU.mult, ["kv", "p2"], ["zb"])
     fill(T.db[:], -18.0, ["db"])
-    fill(T.ws0[:, 0:16], 0.0, ["pad0", "pad2"])
-    fill(T.ws1[:, 0:16], 0.0, ["pad1", "pad3"])
+    for t in range(R):
+        fill(T[snd(t)[0]][:, 0:16], 0.0, ["pad%d0" % t, "pad%d2" % t])
+        fill(T[snd(t)[1]][:, 0:16], 0.0, ["pad%d1" % t, "pad%d3" % t])
     fill(T.df[:, 8:A:8], 14.0, ["df"])
     quant("e", 0, 128, T.zb[:, 3:515], ["zb"], ["e0"])
     ts(T.m1[:], T.a1[:], pf(S1), 2048.0, ALU.is_ge, ALU.mult, ["a1", "s1"], ["m1"])
@@ -309,8 +328,8 @@ def rank_program(g, core, T, topo):
         mm(bank, [("e", 128 * b, name, a, n)], r + ["e%d" % b])
 
     def slots(eng, t, o):
-        gather(eng, o, T["bt%d" % t][:, o:4 * A:2], snd, 16 + 2 * A, T["lnd%d" % t][:, 0:S], ["LL%d" % t],
-               ["pad", "ts"], "bt%d" % t)
+        gather(eng, o, T["bt%d" % t][:, o:4 * A:2], snd(t), 16 + 2 * A, T["lnd%d" % t][:, 0:S], ["LL%d" % t],
+               ["pad%d" % t, "ts%d" % t], "bt%d" % t)
 
     eng_of = lambda b: "A" if b & 1 else "V"
     order = (1, 0, 3, 2)
@@ -384,7 +403,7 @@ def rank_program(g, core, T, topo):
         unpack(bank[b], b, "l0", 0, A, ["LQ0"])
     cuts(1, 4)
     for b in order:
-        out_of(eng_of(b), bank[b], snd, 16, b, A, "ts")
+        out_of(eng_of(b), bank[b], snd(0), 16, b, A, "ts0")
     slots("A", 0, 1)
     slots("V", 0, 0)
     refill(0, {1: 2, 3: 3, 0: 4, 2: 5})
@@ -402,7 +421,7 @@ def rank_program(g, core, T, topo):
     send_top(2)
     scores(2, 0, 1)
     for b in range(4):
-        out_of("A", 4 + b, snd, 16, b, A, "ts")
+        out_of("A", 4 + b, snd(1), 16, b, A, "ts1")
     signs(2, 0, 1)
     cones(2, 2)
     slots("A", 1, 0)
@@ -424,7 +443,7 @@ def rank_program(g, core, T, topo):
         unpack(low[b], b, "x2", A, A, bot(2))
     tt(T.oab[:, 0:S], ow(2, GP), c0, ALU.subtract, ["gp2", "kv"], ["oa0"])
     for b in order:
-        out_of(eng_of(b), bank[b], snd, 16, b, A, "ts")
+        out_of(eng_of(b), bank[b], snd(2), 16, b, A, "ts2")
     slots("A", 2, 1)
     slots("V", 2, 0)
     for b in late:
@@ -449,4 +468,4 @@ def rank_program(g, core, T, topo):
     for k in range(4):
         op("S", lambda k=k: g.sync.dma_start(T.osc[4 * k:4 * k + 4, :], T.sx3[32 * k:32 * k + 4, :]), ["q30", "q31"], [], "stS")
 
-    _schedule(g, T, ops, arrivals, extra)
+    _schedule(g, T, [ops[i] for i in ORDER], arrivals, extra)

@@ -3,24 +3,30 @@ from concourse.mybir import dt, AluOpType, ActivationFunctionType
 ALU = AluOpType
 ACT = ActivationFunctionType
 S, E, A, C, R = 20, 8, 160, 320, 3
-BF, F32, I32, U16, MXC, MXS = "bfloat16", "float32", "int32", "uint16", "float8_e4m3fn_x4", "uint8"
+BF, F32, U16, MXC, MXS = "bfloat16", "float32", "uint16", "float8_e4m3fn_x4", "uint8"
 SMALL = 0.015625
-CUT, CUT2 = 12, 8
+NE = E + 1
+NC = NE * S
+GA, GC, G0 = 49, 384, 1200
+OWN0, OWN = 54, 1112
+FAR0, FAR = 32, 672
+BIG = 32768.0
+HOOK = []
+CUT = {"x": 13, "top0": 20, "top1": 14, "low0": 12, "low1": 20, "B0": 20, "B1": 20, "B2": 20, "end0": 14, "end1": 8}
+ORDER = """
+ijp ldx zzb ldu ia2 zb zft qE3 ilu qE0 ip zct ia1 zF0 xtb xta ldwc ldws p2 p8 qT0 pu s2 lu s1 dd1 xb* qu0 ss0 m2 urq urs
+m1 qL0 u48 p16 m3 mQ0 mP0 pq mT00 oQ0 mL00 oP0 ct1 qE1 oT00 ct0 sq0 qE2 mT01 down dd0 mL03 qf0 ivv mT02 qcone oT01 oL00*
+mC0 zH1 mT03 mL01 oC0 mL02 oT03 oT02* fw0 down1 up oL03 bw0 oL01* oL02 sg0 lt0 zF1 gtop0a gtop0b zH0 mF03 qT1 mF01 ra0
+mF00 oF03 mQ1 oF01 mP1 oF00 mF02 oQ1 mT11 oP1 mT13 rb0 oF02* ls0 cown qf1 gB0b gB0a mC1 mT12 mT10 oT13 oC1 oT12* qB0
+oT11 fw1 rc0 oT10* mH01 bw1 rd0 mH00 ls1 sg1 lx0 ra1 oH01 mH02 gB1b* gB1a* mH03 oH02 oH00* oH03* qB1 glow0c glow0b*
+glow0a* sq1 ss1 qL1 rb1 lt1 mL12 mL10 mL11 oL12* mL13 oL10 oL11* oL13 gtop1c* gtop1a* gtop1b* qT2 rc1 mP2 ss2 mQ2 mT21
+sq2 oP2 oQ2 qf2 mC2 mH10 oC2 mH13 mH11 fw2 mH12 bw2 rd1 oH11 mT22 oa0 sg2 lx1 oH13 mT23 oH10 oH12* oa1 oT21 stoa glow1b
+glow1a ldv mF21 mF20 qL2 mF23 oF21* mF22 oF20* mL21 oF23* mL22 oF22* mL23 ls2 mT20 ra2 mL20 gB2b* gB2a* lt2 oL22* rb2
+oT20* qB2 oL20* rc2 oT23 mH21 oL23 rd2 mH23 lx2 oL21* oH21 mH20 oT22 qv0 oH23 mH22 oH20* gend1b* oH22* gend0b gend1c*
+gend0a gend1a* gend0c qX1 qX0 mY1 stc1 stc0 mY0 sts1 sts0 oY1 sts2 sts3 oY0 sty
+"""
 
-SWAP = (95, 112, 135, 136, 137, 138, 139, 150, 153, 208, 209, 216, 226)
-ORDER = (33, 16, 4, 12, 10, 30, 11, 36, 13, 5, 14, 15, 9, 0, 17, 34, 19, 6, 18, 7, 8, 29, 39, 26, 38, 40, 41, 1, 42, 27,
-         43, 21, 46, 28, 47, 48, 44, 52, 37, 23, 54, 49, 22, 20, 53, 55, 24, 57, 59, 56, 60, 51, 58, 61, 62, 25, 66, 67,
-         70, 45, 63, 71, 72, 73, 74, 75, 64, 77, 78, 80, 76, 68, 81, 79, 50, 65, 84, 69, 82, 86, 85, 87, 94, 32, 92, 31,
-         90, 95, 96, 91, 105, 93, 104, 107, 97, 3, 2, 114, 83, 112, 88, 98, 117, 111, 106, 99, 116, 113, 108, 115, 100,
-         102, 101, 118, 123, 109, 103, 125, 110, 127, 119, 89, 124, 120, 140, 126, 128, 121, 129, 122, 133, 130, 134,
-         131, 156, 157, 135, 136, 137, 155, 154, 138, 139, 166, 141, 142, 35, 144, 132, 147, 146, 168, 148, 165, 167,
-         153, 150, 149, 152, 145, 151, 159, 158, 160, 164, 163, 192, 170, 174, 181, 169, 179, 171, 175, 173, 172, 198,
-         193, 177, 183, 182, 195, 176, 200, 197, 184, 178, 196, 194, 207, 202, 185, 208, 204, 186, 162, 187, 161, 188,
-         143, 210, 211, 209, 189, 190, 199, 206, 180, 222, 214, 212, 215, 213, 201, 191, 216, 203, 223, 224, 205, 226,
-         225, 217, 228, 219, 221, 227, 234, 220, 233, 218, 239, 231, 235, 241, 230, 236, 232, 240, 229, 244, 242, 243,
-         237, 238, 246, 247, 245, 250, 248, 251, 249, 252, 257, 253, 255, 254, 261, 256, 258, 260, 259, 265, 264, 266,
-         262, 267, 263)
-SCRATCH = {}
+SCRATCH = {"xin": ("sbuf", [128, S, 64], BF)}
 
 
 def _sb(name, n, d):
@@ -32,21 +38,22 @@ def _mx(name, n):
     _sb("s" + name, n, MXS)
 
 
-for _n, _w, _d in [("xin", 4 * C, BF), ("uin", 512, BF), ("vin", 512, BF), ("ft", 512, BF), ("ct", 4 * A, BF),
-                   ("zb", 516, BF), ("pi", 8, I32), ("pf", 16, F32), ("kv", 192, F32), ("a1", 192, BF), ("a2", 192, BF),
-                   ("m1", 192, BF), ("m2", 192, BF), ("m3", 192, BF), ("cc", 3 * S, F32), ("df", A, BF), ("db", S, BF),
-                   ("lp", 32, U16), ("yb", C, F32), ("oab", 2 * S, F32), ("lf", 2 * S, U16)]:
+for _n, _w, _d in [("xh", 4 * C, BF), ("uin", 512, BF), ("vin", 512, BF), ("ft", 512, BF), ("ct", 4 * NC, BF),
+                   ("zb", 516, BF), ("pf", 16, F32), ("pb", 8, BF), ("jp", 128, BF), ("a1", 216, BF), ("a2", 216, BF),
+                   ("m1", 216, BF), ("m2", 216, BF), ("m3", 216, BF), ("vv", NC, F32), ("cown", S, F32),
+                   ("dd", 2 * S, F32), ("lu0", 8, F32), ("lu", 8, U16), ("yb", C, F32), ("oab", 2 * S, F32),
+                   ("lf", 2 * S, U16), ("fa", FAR, BF), ("fb", FAR, BF)]:
     _sb(_n, _w, _d)
-for _n, _w in [("w", 512), ("u", 128), ("ur", 128), ("v", 128), ("xn", C), ("c", A), ("e", 512), ("x3", C)]:
+for _n, _w in [("w", 512), ("u", 128), ("ur", 128), ("v", 128), ("c", NC), ("e", 512), ("x3", C), ("o1", A)]:
     _mx(_n, _w)
 for _t in range(R):
     _mx("x%d" % _t, C)
-    _mx("l%d" % _t, A)
     _mx("b%d" % _t, A)
     _mx("f%d" % _t, 128)
-    for _n, _w, _d in [("xs", 4 * C, BF), ("bt", 4 * A, BF), ("wa", 6 * A, BF), ("wb", 6 * A, BF), ("val", A, BF),
-                       ("pa", 16 + 2 * A, BF), ("pb", 16 + 2 * A, BF),
-                       ("fw", A, BF), ("ow", 7 * S, F32), ("rx", 4 * S, F32), ("snd", 2 * S, U16), ("lnd", 2 * S, U16)]:
+    if _t != 1:
+        _mx("l%d" % _t, A)
+    for _n, _w, _d in [("xs", 4 * C, BF), ("bt", 4 * A, BF), ("wa", OWN, BF), ("wb", OWN, BF), ("d", NC, F32),
+                       ("fw", S, F32), ("g", S, F32), ("rx", 4 * S, F32), ("lnd", S, F32), ("ls", S, U16)]:
         _sb(_n + str(_t), _w, _d)
 for _t in range(R - 1):
     _sb("lt%d" % _t, S, U16)
@@ -58,14 +65,26 @@ SEMAPHORES = (["cV", "cA", "cP", "cG", "dx", "du", "dw", "dv", "stS", "stA", "go
               + ["rq%d" % t for t in range(R)] + ["rl%d" % t for t in range(R)])
 
 
-def _schedule(g, T, ops, arrivals, extra):
+def _schedule(g, T, ops, arrivals, extra, bank):
     queue = {"V": g.vector, "A": g.scalar, "P": g.tensor, "G": g, "S": g.sync}
     writer, readers, deps = dict(arrivals), {}, []
     marked = set()
-    for i, (eng, fn, r, w, sem) in enumerate(ops):
+    free = list(range(8))
+    for i, (name, eng, fn, r, w, sem) in enumerate(ops):
+        w = list(w)
+        for k in list(w):
+            if k[0] in "+-":
+                if k[0] == "+":
+                    bank[k[1:]] = free.pop(0)
+                else:
+                    free.append(bank[k[1:]])
+                w[w.index(k)] = "bank%d" % bank[k[1:]]
         d = []
         for k in r:
-            d.append(writer[k])
+            if k[0] != "?":
+                d.append(writer[k])
+            elif k[1:] in writer:
+                d.append(writer[k[1:]])
         for k in w:
             if k in writer:
                 d.append(writer[k])
@@ -76,18 +95,18 @@ def _schedule(g, T, ops, arrivals, extra):
             if isinstance(x, int):
                 marked.add(x)
         for k in r:
-            readers.setdefault(k, []).append(i)
+            readers.setdefault(k.lstrip("?"), []).append(i)
         for k in w:
             writer[k] = i
             readers[k] = []
     total = dict(extra)
     shared = {}
-    for eng, fn, r, w, sem in ops:
+    for name, eng, fn, r, w, sem in ops:
         if sem is not None:
             shared[sem] = shared.get(sem, 0) + 16
     know = {e: {} for e in queue}
     done, waited = {}, {}
-    for i, (eng, fn, r, w, sem) in enumerate(ops):
+    for i, (name, eng, fn, r, w, sem) in enumerate(ops):
         local = sorted(set(x for x in deps[i] if isinstance(x, int)), reverse=True)
         need = [done[x] for x in local] + [(x[0], x[1], {}) for x in deps[i] if not isinstance(x, int)]
         for s, v, kn in need:
@@ -98,7 +117,7 @@ def _schedule(g, T, ops, arrivals, extra):
             know[eng][s] = v
             for s2, v2 in kn.items():
                 know[eng][s2] = max(know[eng].get(s2, 0), v2)
-        ins = fn()
+        ins = fn(eng)
         if sem is not None:
             ins.then_inc(T.sem[sem], 16)
             total[sem] = shared[sem]
@@ -120,10 +139,10 @@ def rank_program(g, core, T, topo):
         return
     n_ranks = len(T.cores)
     V, SC, PE = g.vector, g.scalar, g.tensor
-    ops = []
+    ops, bank = [], {}
 
-    def op(eng, fn, r, w, sem=None):
-        ops.append((eng, fn, r, w, sem))
+    def op(name, eng, fn, r, w, sem=None):
+        ops.append((name, eng, fn, r, w, sem))
 
     common = set.intersection(*[set(topo.engines(a, b)) for a in T.cores for b in T.cores if a != b])
     mask, ne = sum(1 << e for e in common), len(common)
@@ -135,337 +154,216 @@ def rank_program(g, core, T, topo):
         extra["rq%d" % t] = 2 * ne
         extra["rl%d" % t] = ne
 
-    def send(t, out, in_, sem, r):
+    def send(name, t, out, in_, sem, r):
         dst = T.cores[(rank + 1 + t) % n_ranks]
         rid, pid = topo.addr(dst, core)
         extra["gone"] += ne
-        op("G", lambda: g.remote_dma(out, in_, T.sem[sem], T.sem.gone, pid, rid, mask), r, [])
+        op(name, "G", lambda e: g.remote_dma(out, in_, T.sem[sem], T.sem.gone, pid, rid, mask), r, [])
 
-    def other(eng):
-        return {"V": "A", "A": "V"}[eng] if len(ops) in SWAP else eng
+    def load(name, out, in_, r, w, sem):
+        op(name, "S", lambda e: g.sync.dma_start(out, in_), r, w, sem)
 
-    def ts(out, in0, s1, s2, o0, o1, r, w):
+    def ts(name, out, in0, s1, s2, o0, o1, r, w):
         if o1 is None:
-            op("V", lambda: V.tensor_scalar(out, in0, s1, None, o0), r, w)
+            op(name, "V", lambda e: V.tensor_scalar(out, in0, s1, None, o0), r, w)
         else:
-            op("V", lambda: V.tensor_scalar(out, in0, s1, s2, o0, o1), r, w)
+            op(name, "V", lambda e: V.tensor_scalar(out, in0, s1, s2, o0, o1), r, w)
 
-    def tt(out, a, b, o, r, w):
-        op("V", lambda: V.tensor_tensor(out, a, b, o), r, w)
+    def tt(name, out, a, b, o, r, w):
+        op(name, "V", lambda e: V.tensor_tensor(out, a, b, o), r, w)
 
-    def cp(out, in_, r, w):
-        op("V", lambda: V.tensor_copy(out, in_), r, w)
+    def fill(name, ap, c, w):
+        op(name, "V", lambda e: V.memset(ap, c), [], w)
 
-    def fill(ap, c, w):
-        op("V", lambda: V.memset(ap, c), [], w)
+    def iota(name, out, pattern, base, step, w):
+        op(name, "G", lambda e: g.iota(out, pattern, base, step, allow_small_or_imprecise_dtypes=True), [], w)
 
-    def act(out, in_, func, r, w, **kw):
-        op("A", lambda: SC.activation(out, in_, func, **kw), r, w)
+    def act(name, out, in_, func, r, w, **kw):
+        op(name, "A", lambda e: SC.activation(out, in_, func, **kw), r, w)
+
+    def copy(name, eng, out, in_, r, w):
+        op(name, eng, lambda e: V.tensor_copy(out, in_) if e == "V" else SC.activation(out, in_, ACT.Copy), r, w)
 
     def quant(name, a, b, in_, r, w):
-        op("V", lambda: V.quantize_mx(T["q" + name][:, a:b], T["s" + name][:, a:b], in_), r, w)
+        op("q" + w, "V", lambda e: V.quantize_mx(T["q" + name][:, a:b], T["s" + name][:, a:b], in_), r, [w])
 
-    def pick(dst, a, b, src, n, off, r, wq, wsc):
-        op("V", lambda: V.tensor_copy(T["q" + dst][:, a:b].bitcast(dt.uint32),
-                                      T["q" + src][:, 0:n].bitcast(dt.uint32).indirect(off)), r, [wq])
-        op("A", lambda: SC.activation(T["s" + dst][:, a:b], T["s" + src][:, 0:n].indirect(off), ACT.Copy), r, [wsc])
+    ps = lambda name: T["ps%d" % bank[name]]
 
-    def mm(bank, terms, r):
-        def fn():
+    def mm(name, terms, r):
+        def fn(e):
             ins = None
             for i, (ln, la, rn, ra, n) in enumerate(terms):
-                ins = PE.matmul_mx(T["ps%d" % bank][:, 0:n], T["q" + ln][:, la:la + 128], T["s" + ln][:, la:la + 128],
+                ins = PE.matmul_mx(ps(name)[:, 0:n], T["q" + ln][:, la:la + 128], T["s" + ln][:, la:la + 128],
                                    T["q" + rn][:, ra:ra + n], T["s" + rn][:, ra:ra + n], i == 0, i == len(terms) - 1)
             return ins
-        op("P", fn, r, ["B%d" % bank])
+        op("m" + name, "P", fn, r, ["+" + name])
 
-    def out_of(eng, bank, win, base, b, n, *keys):
-        dst = T[win[b & 1]][:, base + (b >> 1):base + 2 * n:2]
-        src = T["ps%d" % bank][:, 0:n]
-        w = ["B%d" % bank] + [k + str(b) for k in keys]
-        eng = other(eng)
-        if eng == "V":
-            ts(dst, src, SMALL, None, ALU.mult, None, [], w)
-        else:
-            act(dst, src, ACT.Copy, [], w, scale=SMALL)
-
-    def gather(eng, o, out, win, n, off, r, keys, w):
-        src = T[win[o]][:, 0:n].indirect(off)
-        rr = r + [k + str(b) for k in keys for b in (o, o + 2)]
-        eng = other(eng)
-        if eng == "V":
-            cp(out, src, rr, [w + str(o)])
-        else:
-            act(out, src, ACT.Copy, rr, [w + str(o)])
+    def out_of(name, eng, dst, scale, w):
+        def fn(e):
+            src = ps(name)[:, 0:A]
+            return (V.tensor_scalar(dst, src, scale, None, ALU.mult) if e == "V"
+                    else SC.activation(dst, src, ACT.Copy, scale=scale))
+        op("o" + name, eng, fn, [], ["-" + name, w])
 
     pf = lambda j: T.pf[:, j:j + 1]
-    P_, K2, Q_, Q8, CP, S1, S2, P2, P1, Q320, NK2 = range(11)
-    own = lambda t: ("wa%d" % t, "wb%d" % t)
-    snd = lambda t: ("pa%d" % t, "pb%d" % t)
-
-    op("S", lambda: g.sync.dma_start(T.xin[:], T.x[:]), [], ["xin"], "dx")
-    op("S", lambda: g.sync.dma_start(T.uin[:], T.u[:]), [], ["uin"], "du")
-    op("S", lambda: g.sync.dma_start(T.qw[:].bitcast(dt.uint8), T.wc[:]), ["xin"], ["qw"], "dw")
-    op("S", lambda: g.sync.dma_start(T.sw[:], T.ws[:]), [], ["sw"], "dw")
-
-    flag = dict(allow_small_or_imprecise_dtypes=True)
-    op("G", lambda: g.iota(T.pi[:, 0:1], [[1, 1]], 0, 1), [], ["pi0"])
-    op("G", lambda: g.iota(T.kv[:], [[2, 192]], 0, 0, **flag), [], ["kv"])
-    op("G", lambda: g.iota(T.a1[:], [[-1, 24], [1, E]], 4, -1, **flag), [], ["a1"])
-    op("G", lambda: g.iota(T.a2[:], [[1, 24], [1, E]], -4, -1, **flag), [], ["a2"])
-    op("G", lambda: g.iota(T.ft[:], [[0, 512]], 0, 0, **flag), [], ["ft0", "ft1"])
-    fill(T.ct[:], 0.0, ["ct0", "ct1"])
-    for j, (o, s) in enumerate([(ALU.bitwise_and, 14), (ALU.bitwise_and, 15), (ALU.bitwise_and, 8),
-                                (ALU.arith_shift_right, 3)]):
-        ts(T.pi[:, j + 1:j + 2], T.pi[:, 0:1], s, None, o, None, ["pi0"], ["pi%d" % (j + 1)])
-    fill(T.zb[:], 0.0, ["zb"])
-    cp(T.pf[:, 0:5], T.pi[:, 0:5], ["pi%d" % j for j in range(5)], ["pf"])
-    fill(T.df[:], 0.0, ["df"])
-    act(pf(P2), pf(P_), ACT.Copy, ["pf"], ["p2"], scale=2.0)
-    act(pf(S1), pf(CP), ACT.Copy, ["pf"], ["s1"], scale=-9.0)
-    act(pf(S2), pf(CP), ACT.Copy, ["pf"], ["s2"], scale=-7.0)
-    act(pf(P1), pf(K2), ACT.Identity, ["pf"], ["p1"], scale=-2.0, bias=pf(Q_))
-    act(pf(NK2), pf(K2), ACT.Copy, ["pf"], ["nk2"], scale=-1.0)
-    act(pf(Q320), pf(Q_), ACT.Identity, ["pf", "kv"], ["q320"], bias=T.kv[:, A:A + 1])
-    c0 = T.kv[:, 0:A:8]
-    cK, cN, cOwn = T.cc[:, 0:S], T.cc[:, S:2 * S], T.cc[:, 2 * S:3 * S]
-    act(cK, c0, ACT.Identity, ["kv", "pf"], ["cK"], bias=pf(K2))
-    act(cN, T.kv[:, 8:8 + A:8], ACT.Identity, ["kv", "nk2"], ["cN"], bias=pf(NK2))
-    act(cOwn, T.kv[:, 7:7 + A:8], ACT.Identity, ["kv", "p1"], ["cOwn"], bias=pf(P1))
-    cp(T.lp[:, 0:8], T.kv[:, 0:64:8], ["kv"], ["lu"])
-    ts(T.lp[:, 8:18], T.kv[:, 0:A:16], pf(Q_), pf(Q8), ALU.add, ALU.add, ["kv", "pf"], ["lpt"])
-    ts(T.lp[:, 18:28], T.kv[:, 4:4 + A:16], pf(Q_), pf(Q8), ALU.add, ALU.add, ["kv", "pf"], ["lpb"])
-    ts(T.zb[:, 3:515:4], T.kv[:, 0:128], pf(P2), 64.0, ALU.is_equal, ALU.mult, ["kv", "p2"], ["zb"])
-    fill(T.db[:], -18.0, ["db"])
-    for t in range(R):
-        fill(T[snd(t)[0]][:, 0:16], 0.0, ["pad%d0" % t, "pad%d2" % t])
-        fill(T[snd(t)[1]][:, 0:16], 0.0, ["pad%d1" % t, "pad%d3" % t])
-    fill(T.df[:, 8:A:8], 14.0, ["df"])
-    quant("e", 0, 128, T.zb[:, 3:515], ["zb"], ["e0"])
-    ts(T.m1[:], T.a1[:], pf(S1), 2048.0, ALU.is_ge, ALU.mult, ["a1", "s1"], ["m1"])
-    ts(T.m2[:], T.a2[:], pf(S2), None, ALU.is_ge, None, ["a2", "s2"], ["m2"])
-    quant("e", 128, 256, T.zb[:, 2:514], ["zb"], ["e1"])
-    tt(T.m3[:], T.m1[:], T.m2[:], ALU.mult, ["m1", "m2"], ["m3"])
-    act(T.ct[:, 0:4 * A:4], T.m3[:, 32:192], ACT.Copy, ["m3"], ["ct0"])
-    act(T.ct[96:128, 1:4 * A:4], T.m3[96:128, 0:A], ACT.Copy, ["m3"], ["ct1"])
-    quant("e", 256, 384, T.zb[:, 1:513], ["zb"], ["e2"])
-
-    top = lambda t: ["qt%d" % t, "st%d" % t]
-    bot = lambda t: ["qb%d" % t, "sb%d" % t]
-
-    def send_top(t):
-        send(t, T["ql%d" % t][:].bitcast(dt.uint8), T["qx%d" % t][:, 0:A].bitcast(dt.uint8), "rq%d" % t, top(t))
-        send(t, T["sl%d" % t][:], T["sx%d" % t][:, 0:A], "rq%d" % t, top(t))
-
-    def scores(t, b0, b1):
-        mm(b0, [("x%d" % t, 0, "ur", 0, 128)], top(t) + ["qur", "sur"])
-        mm(b1, [("x%d" % t, 32, "ur", 0, 128)], top(t) + ["qur", "sur"])
-
-    def signs(t, b0, b1):
-        ts(T.ft[:, 0:512:4], T["ps%d" % b0][:, 0:128], 0.0, 0.5, ALU.is_gt, ALU.subtract, [], ["B%d" % b0, "ft0"])
-        ts(T.ft[96:128, 1:512:4], T["ps%d" % b1][96:128, 0:128], 0.0, 0.5, ALU.is_gt, ALU.subtract, [],
-           ["B%d" % b1, "ft1"])
-        quant("f%d" % t, 0, 128, T.ft[:], ["ft0", "ft1"], ["qf%d" % t])
-
-    def cones(t, b):
-        mm(b, [("f%d" % t, 0, "c", 0, A)], ["qf%d" % t, "cone"])
-
-    ow = lambda t, j: T["ow%d" % t][:, S * j:S * j + S]
-    G_, M_, GP, Y_, N_, N2, A3 = range(7)
-
-    def cuts(t, b):
-        k = str(t)
-        val, fw = T["val" + k], T["fw" + k]
-        tt(val[:], T["ps%d" % b][:, 0:A], T.kv[:, 1:1 + A], ALU.min, ["kv"], ["B%d" % b, "val" + k])
-        op("V", lambda: V.tensor_tensor_scan(fw[:], T.df[:], val[:], 0.0, ALU.add, ALU.max), ["df", "val" + k], ["fw" + k])
-        op("V", lambda: V.tensor_tensor_scan(T["ow" + k][:, S - 1::-1], T.db[:], fw[:, A - 1::-8], -1000.0,
-                                             ALU.add, ALU.max), ["db", "fw" + k], ["g" + k])
-
-    def slot_list(t, j):
-        k = str(t)
-        sl = T["snd" + k]
-        if j == 0:
-            tt(ow(t, M_), ow(t, G_), cK, ALU.is_gt, ["g" + k, "cK"], ["m" + k])
-        elif j == 1:
-            tt(ow(t, GP), ow(t, G_), c0, ALU.max, ["g" + k, "kv"], ["gp" + k])
-        elif j == 2:
-            tt(ow(t, Y_), ow(t, M_), ow(t, G_), ALU.mult, ["m" + k, "g" + k], ["y" + k])
-        elif j == 3:
-            cp(sl[:, S:2 * S], ow(t, GP), ["gp" + k], ["sg" + k])
-        else:
-            ts(sl[:, 0:S], ow(t, Y_), pf(P1), 14.0, ALU.add, ALU.add, ["y" + k, "p1"], ["sl" + k])
-            send(t, T["lnd" + k][:], sl[:], "rl" + k, ["sg" + k, "sl" + k])
-
+    pb = lambda j: T.pb[:, 2 * j:2 * j + 1]
+    P_, S1, S2, Q_, U_, UP, DOWN, DOWN1, U48 = range(9)
     lt = lambda t: T["lt%d" % t][:] if t < R - 1 else T.lf[:, 0:2 * S:2]
     lx = lambda t: T["lx%d" % t][:] if t < R - 1 else T.lf[:, 1:2 * S:2]
 
-    def own_list(t, j):
-        k = str(t)
-        if j == 0:
-            tt(ow(t, N_), ow(t, G_), cN, ALU.is_ge, ["g" + k, "cN"], ["n" + k])
-        elif j == 1:
-            ts(ow(t, N2), ow(t, N_), float(2 * A - 16), pf(Q320), ALU.mult, ALU.add, ["n" + k, "q320"], ["n2" + k])
-        elif j == 2:
-            tt(ow(t, A3), ow(t, GP), ow(t, N2), ALU.add, ["gp" + k, "n2" + k], ["a3" + k])
-        else:
-            ts(lt(t), ow(t, A3), float(-2 * A), None, ALU.add, None, ["a3" + k], ["lt" + k])
+    def plane(win, o):
+        return T[("fa", "fb")[o]] if win == "F" else T[("wa", "wb")[o] + win]
 
-    def refill_list(t, j):
+    def product(name, win, part, terms, r):
+        for b in (1, 3, 0, 2):
+            mm(name + str(b), terms(b), r + ["E%d" % b])
+        for b in (1, 3, 0, 2):
+            if win == "F":
+                first, step = FAR0 + 2 * (b >> 1) + 1, 4
+            else:
+                j = "tbh".index(part)
+                first, step = OWN0 + 6 * E * j + 3 * (b >> 1) + j, 6
+            out_of(name + str(b), "av"[1 - (b & 1)], plane(win, b & 1)[:, first:first + step * (A - 1) + 1:step], SMALL,
+                   win + part + str(b))
+
+    def gather(name, tile, first, win, parts, lst, col, r):
+        made = []
+        for piece, eng, o, a, b in (("b", "a", 1, 0, S), ("a", "v", 0, 0, CUT[name]), ("c", "a", 0, CUT[name], S)):
+            if a < b:
+                keys = [("" if p in parts else "?") + win + p + str(j) for p in "tbhz" for j in (o, o + 2)]
+                copy("g" + name + piece, eng, tile[:, first + 32 * a + o:first + 32 * b:2],
+                     plane(win, o)[:].indirect(lst[:, col + a:col + b]), r + keys, [name + piece])
+                made.append(name + piece)
+        return made
+
+    load("ldx", T.xin[:], T.x[:], [], ["xin"], "dx")
+    load("ldu", T.uin[:], T.u[:], [], ["uin"], "du")
+    load("ldwc", T.qw[:].bitcast(dt.uint8), T.wc[:], ["xin"], ["qw"], "dw")
+    load("ldws", T.sw[:], T.ws[:], ["xin"], ["sw"], "dw")
+
+    iota("ip", pf(P_), [[0, 1]], 0, 1, ["p"])
+    iota("ia1", T.a1[:], [[1, 24], [1, NE]], -S, -1, ["a1"])
+    iota("ia2", T.a2[:], [[-1, 24], [1, NE]], S - 2, -1, ["a2"])
+    iota("ilu", T.lu0[:], [[16, 8]], 0, 0, ["lu0"])
+    iota("ijp", T.jp[:], [[1, 128]], 0, -1, ["jp"])
+    iota("ivv", T.vv[:], [[-GC, S], [GA, NE]], G0 + GC * (S - 1), 0, ["vv"])
+    fill("zct", T.ct[:], 0.0, ["ct0", "ct1"])
+    fill("zft", T.ft[:], 0.0, ["ft"])
+    fill("zzb", T.zb[:], 0.0, ["zb"])
+    fill("dd0", T.dd[:, 0:S], float(-GC - GA), ["dd0"])
+    fill("dd1", T.dd[:, S:2 * S], float(GC - GA), ["dd1"])
+    act("p8", pb(0), pf(P_), ACT.Copy, ["p"], ["p8"], bias=1280 - 3.5)
+    act("p16", pb(1), pf(P_), ACT.Copy, ["p"], ["p16"], bias=2560 - 7.5)
+    act("p2", pb(2), pf(P_), ACT.Copy, ["p"], ["p2"], bias=320 - 0.5)
+    act("s1", pf(S1), pb(0), ACT.Copy, ["p8"], ["s1"], scale=-1.125, bias=1440.0)
+    act("s2", pf(S2), pb(0), ACT.Copy, ["p8"], ["s2"], scale=-0.875, bias=1120.0)
+    act("pq", pf(Q_), pb(1), ACT.Identity, ["p16", "p"], ["q"], scale=-1.0, bias=pf(P_))
+    act("pu", pf(U_), pb(2), ACT.Identity, ["p2", "p"], ["u"], scale=-1.0, bias=pf(P_))
+    act("up", pf(UP), pf(Q_), ACT.Copy, ["q"], ["up"], scale=24.5, bias=24.5 * 2560 - 3.75 - G0 + E * OWN0)
+    act("u48", pf(U48), pf(U_), ACT.Copy, ["u"], ["u48"], scale=48.5,
+        bias=48.5 * 320 - 24.5 * 2560 - G0 - GA + 12 * FAR0 + 6.5)
+    act("down", pf(DOWN), pf(Q_), ACT.Identity, ["q", "u48"], ["down"], scale=-24.5, bias=pf(U48))
+    act("down1", pf(DOWN1), pf(DOWN), ACT.Copy, ["down"], ["down1"], bias=E * OWN0 - 3.5 - 12 * FAR0 - 6.5)
+    act("cown", T.cown[:], T.vv[:, NC - 1::-NE], ACT.Identity, ["vv", "down1"], ["cown"], bias=pf(DOWN1))
+    ts("m1", T.m1[:], T.a1[:], pf(S1), BIG, ALU.is_ge, ALU.mult, ["a1", "s1"], ["m1"])
+    ts("m2", T.m2[:], T.a2[:], pf(S2), None, ALU.is_ge, None, ["a2", "s2"], ["m2"])
+    tt("m3", T.m3[:], T.m1[:], T.m2[:], ALU.mult, ["m1", "m2"], ["m3"])
+    act("ct0", T.ct[:, 0:4 * NC:4], T.m3[:, 0:NC], ACT.Copy, ["m3"], ["ct0"])
+    act("ct1", T.ct[96:128, 1:4 * NC:4], T.m3[96:128, 4 * NE:4 * NE + NC], ACT.Copy, ["m3"], ["ct1"], scale=0.5)
+    quant("c", 0, NC, T.ct[:], ["ct0", "ct1"], "cone")
+    copy("lu", "V", T.lu[:], T.lu0[:], ["lu0"], ["lu"])
+    ts("zb", T.zb[:, 3:515:4], T.jp[:], 0.0, 64.0, ALU.is_equal, ALU.mult, ["jp"], ["zb"])
+    for b in range(4):
+        quant("e", 128 * b, 128 * b + 128, T.zb[:, 3 - b:515 - b], ["zb"], "E%d" % b)
+    for o in (0, 1):
+        iota("zF%d" % o, plane("F", o)[:, 0:4 * A:2], [[0, 2 * A]], 0, 0, ["Fz%d" % o, "Fz%d" % (o + 2)])
+        iota("zH%d" % o, plane("1", o)[:, 5:963:3], [[0, 2 * A]], 0, 0, ["1h%d" % o, "1h%d" % (o + 2)])
+
+    copy("xtb", "a", T.xh[:, 32 * CUT["x"]:4 * A], T.xin[:, CUT["x"]:S, 0:32], ["xin"], ["xtb"])
+    copy("xta", "v", T.xh[:, 0:32 * CUT["x"]], T.xin[:, 0:CUT["x"], 0:32], ["xin"], ["xta"])
+    quant("x0", 0, A, T.xh[:, 0:4 * A], ["xta", "xtb"], "T0")
+    copy("xb", "v", T.xh[:, 4 * A:8 * A], T.xin[:, :, 32:64], ["xin"], ["xb"])
+    quant("x0", A, C, T.xh[:, 4 * A:8 * A], ["xb"], "L0")
+    quant("u", 0, 128, T.uin[:], ["uin"], "u0")
+    op("urq", "V", lambda e: V.tensor_copy(T.qur[:].bitcast(dt.uint32), T.qu[:].bitcast(dt.uint32).indirect(T.lu[:])),
+       ["u0", "lu"], ["qur"])
+    copy("urs", "a", T.sur[:], T.su[:].indirect(T.lu[:]), ["u0", "lu"], ["sur"])
+
+    for t in range(R):
         k = str(t)
+        x, gg, lnd = "x" + k, T["g" + k], T["lnd" + k]
         rx = lambda i: T["rx" + k][:, S * i:S * i + S]
-        if j == 0:
-            ts(rx(0), T["lnd" + k][:, S:2 * S], pf(K2), 16.0, ALU.subtract, ALU.add, ["LL" + k, "pf"], ["r0" + k])
-        elif j == 1:
-            tt(rx(1), rx(0), ow(t, GP), ALU.is_gt, ["r0" + k, "gp" + k], ["r1" + k])
-        elif j == 2:
-            tt(rx(2), rx(1), ow(t, A3), ALU.mult, ["r1" + k, "a3" + k], ["r2" + k])
-        elif j == 3:
-            tt(rx(3), rx(2), cOwn, ALU.max, ["r2" + k, "cOwn"], ["r3" + k])
+        if t != 1:
+            send("sq" + k, t, T["ql" + k][:].bitcast(dt.uint8), T["q" + x][:, 0:A].bitcast(dt.uint8), "rq" + k, ["T" + k])
+            send("ss" + k, t, T["sl" + k][:], T["s" + x][:, 0:A], "rq" + k, ["T" + k])
+        mm("P" + k, [(x, 0, "ur", 0, 128)], ["T" + k, "qur", "sur"])
+        mm("Q" + k, [(x, 32, "ur", 0, 128)], ["T" + k, "qur", "sur"])
+        op("oP" + k, "V", lambda e, k=k: V.tensor_scalar(T.ft[:, 0:512:4], ps("P" + k)[:, 0:128], 0.0, 0.5, ALU.is_gt,
+                                                         ALU.subtract), ["ft"], ["-P" + k, "ft0"])
+        op("oQ" + k, "A", lambda e, k=k: SC.activation(T.ft[96:128, 1:512:4], ps("Q" + k)[96:128, 0:128], ACT.Sign,
+                                                       bias=-2.0 ** -126), ["ft"], ["-Q" + k, "ft1"])
+        quant("f" + k, 0, 128, T.ft[:], ["ft0", "ft1"], "f" + k)
+        mm("C" + k, [("f" + k, 0, "c", 0, NC)], ["f" + k, "cone"])
+        op("oC" + k, "V", lambda e, k=k: V.tensor_tensor_scan(T["d" + k][:], ps("C" + k)[:, 0:NC], T.vv[:], BIG, ALU.max,
+                                                              ALU.min), ["vv"], ["-C" + k, "d" + k])
+        op("fw" + k, "V", lambda e, k=k: V.tensor_tensor_scan(T["fw" + k][:], T.dd[:, 0:S], T["d" + k][:, E:NC:NE], 0.0,
+                                                              ALU.add, ALU.max), ["dd0", "d" + k], ["fw" + k])
+        op("bw" + k, "V", lambda e, k=k: V.tensor_tensor_scan(T["g" + k][:], T.dd[:, S:2 * S], T["fw" + k][:, S - 1::-1],
+                                                              -BIG, ALU.add, ALU.max), ["dd1", "fw" + k], ["g" + k])
+        send("sg" + k, t, lnd[:], gg[:], "rl" + k, ["g" + k])
+        product("T" + k, k, "t", lambda b: [("e", 128 * b, x, 0, A)], ["T" + k])
+        if t == 1:
+            ts("ls1", T.ls1[:], gg[:], pf(DOWN1), 0.125, ALU.add, ALU.mult, ["g1", "down1"], ["ls1"])
+            quant("o1", 0, A, T.bt1[:], gather("B1", T.bt1, 0, "1", "th", T.ls1, 0, ["ls1"]), "B1")
+            send("sq1", t, T.qb1[:].bitcast(dt.uint8), T.qo1[:].bitcast(dt.uint8), "rq1", ["B1"])
+            send("ss1", t, T.sb1[:], T.so1[:], "rq1", ["B1"])
         else:
-            cp(lx(t), rx(3), ["r3" + k], ["lx" + k])
+            product("F" + k, "F", "t", lambda b: [("e", 128 * b, "l" + k, 0, A)], ["LQ" + k])
+            ts("ls" + k, T["ls" + k][:], lnd[:], pf(DOWN), 1.0 / 12, ALU.add, ALU.mult, ["LL" + k, "down"], ["ls" + k])
+            quant("b" + k, 0, A, T["bt" + k][:], gather("B" + k, T["bt" + k], 0, "F", "tz", T["ls" + k], 0, ["ls" + k]),
+                  "B" + k)
+        product("L" + k, k, "b", lambda b: [("e", 128 * b, x, A, A)], ["L" + k])
+        ts("lt" + k, lt(t), gg[:], pf(UP), 0.125, ALU.add, ALU.mult, ["g" + k, "up"], ["lt" + k])
+        ts("ra" + k, rx(0), gg[:], pf(UP), float(GA * E), ALU.add, ALU.add, ["g" + k, "up"], ["ra" + k])
+        tt("rb" + k, rx(1), lnd[:], rx(0), ALU.is_gt, ["LL" + k, "ra" + k], ["rb" + k])
+        tt("rc" + k, rx(2), rx(1), rx(0), ALU.mult, ["rb" + k, "ra" + k], ["rc" + k])
+        tt("rd" + k, rx(3), rx(2), T.cown[:], ALU.max, ["rc" + k, "cown"], ["rd" + k])
+        ts("lx" + k, lx(t), rx(3), 0.125, None, ALU.mult, None, ["rd" + k], ["lx" + k])
+        if t < R - 1:
+            n = str(t + 1)
+            quant("x" + n, 0, A, T["xs" + k][:, 0:4 * A],
+                  gather("top" + k, T["xs" + k], 0, k, "tb", T["lt" + k], 0, ["lt" + k]), "T" + n)
+        product("H" + k, k, "h", lambda b: [("w", 128 * b, "b" + k, 0, A), ("e", 128 * b, "b" + k, 0, A)],
+                ["LQ1" if t == 1 else "B" + k, "qw", "sw"])
+        if t < R - 1:
+            quant("x" + n, A, C, T["xs" + k][:, 4 * A:8 * A],
+                  gather("low" + k, T["xs" + k], 4 * A, k, "tbh", T["lx" + k], 0, ["lx" + k]), "L" + n)
 
-    def unpack(bank, b, name, a, n, r):
-        mm(bank, [("e", 128 * b, name, a, n)], r + ["e%d" % b])
-
-    def slots(eng, t, o):
-        gather(eng, o, T["bt%d" % t][:, o:4 * A:2], snd(t), 16 + 2 * A, T["lnd%d" % t][:, 0:S], ["LL%d" % t],
-               ["pad%d" % t, "ts%d" % t], "bt%d" % t)
-
-    eng_of = lambda b: "A" if b & 1 else "V"
-    order = (1, 0, 3, 2)
-    late = (1, 3, 0, 2)
-
-    def refill(t, bank):
-        refill_list(t, 0)
-        quant("b%d" % t, 0, A, T["bt%d" % t][:], ["bt%d0" % t, "bt%d1" % t], ["qB%d" % t])
-        for b in late:
-            mm(bank[b], [("w", 128 * b, "b%d" % t, 0, A), ("e", 128 * b, "b%d" % t, 0, A)],
-               ["qB%d" % t, "qw", "sw", "e%d" % b])
-        for j in range(4):
-            refill_list(t, j + 1)
-            if t == 0:
-                slot_list(1, j)
-            elif t == 1:
-                own_list(2, j)
-            elif j == 0:
-                quant("v", 0, 128, T.vin[:], ["vin"], ["qv"])
-        if t == 0:
-            slot_list(1, 4)
-        for b in late:
-            out_of(eng_of(b), bank[b], own(t), 4 * A, b, A, "h%d" % t)
-
-    def new_top(t):
-        for eng, o in (("A", 1), ("V", 0)):
-            gather(eng, o, T["xs%d" % t][:, o:4 * A:2], own(t), 4 * A, lt(t), ["lt%d" % t],
-                   ["tt%d" % t, "tb%d" % t], "xt%d" % t)
-        quant("x%d" % (t + 1), 0, A, T["xs%d" % t][:, 0:4 * A], ["xt%d0" % t, "xt%d1" % t], top(t + 1))
-
-    def new_bottom(t):
-        for eng, o, a, b in (("A", 1, 0, S), ("V", 0, 0, CUT), ("A", 0, CUT, S)):
-            gather(eng, o, T["xs%d" % t][:, 4 * A + 32 * a + o:4 * A + 32 * b:2], own(t), 6 * A, T["lx%d" % t][:, a:b],
-                   ["lx%d" % t], ["tt%d" % t, "tb%d" % t, "h%d" % t], "xb%d%s" % (t, eng))
-        if t == 0:
-            own_list(1, 0)
-            own_list(1, 1)
-        quant("x%d" % (t + 1), A, C, T["xs%d" % t][:, 4 * A:8 * A], ["xb%dA0" % t, "xb%dA1" % t, "xb%dV0" % t],
-              bot(t + 1))
-
-    quant("xn", 0, C, T.xin[:], ["xin"], ["qxn"])
-    pick("x0", 0, A, "xn", C, T.lp[:, 8:18], ["qxn", "lpt"], "qt0", "st0")
-    send_top(0)
-    quant("c", 0, A, T.ct[:], ["ct0", "ct1"], ["cone"])
-    quant("u", 0, 128, T.uin[:], ["uin"], ["qu"])
-    pick("ur", 0, 128, "u", 128, T.lp[:, 0:8], ["qu", "lu"], "qur", "sur")
-    scores(0, 4, 5)
-    pick("x0", A, C, "xn", C, T.lp[:, 18:28], ["qxn", "lpb"], "qb0", "sb0")
-    signs(0, 4, 5)
-    for b in range(4):
-        if b == 2:
-            cones(0, 4)
-            quant("e", 384, 512, T.zb[:, 0:512], ["zb"], ["e3"])
-        unpack(b, b, "x0", 0, C, top(0) + bot(0))
-        out_of("A", b, own(0), 0, b, C, "tt0", "tb0")
-    cuts(0, 4)
-    for f, j in ((own_list, 0), (slot_list, 0), (slot_list, 1), (own_list, 1), (slot_list, 2), (slot_list, 3),
-                 (own_list, 2), (slot_list, 4), (own_list, 3)):
-        f(0, j)
-    new_top(0)
-    send_top(1)
-    scores(1, 4, 5)
-    for b in range(4):
-        if b == 2:
-            signs(1, 4, 5)
-            cones(1, 4)
-        unpack(b, b, "x1", 0, A, top(1))
-        out_of("A", b, own(1), 0, b, A, "tt1")
-    bank = {1: 6, 0: 7, 3: 0, 2: 1}
-    for b in order:
-        unpack(bank[b], b, "l0", 0, A, ["LQ0"])
-    cuts(1, 4)
-    for b in order:
-        out_of(eng_of(b), bank[b], snd(0), 16, b, A, "ts0")
-    slots("A", 0, 1)
-    slots("V", 0, 0)
-    refill(0, {1: 2, 3: 3, 0: 4, 2: 5})
-    new_bottom(0)
-    op("S", lambda: g.sync.dma_start(T.vin[:], T.v[:]), bot(1), ["vin"], "dv")
-    for b in order:
-        unpack(b, b, "x1", A, A, bot(1))
-    own_list(1, 2)
-    own_list(1, 3)
-    for b in order:
-        out_of(eng_of(b), b, own(1), 2 * A, b, A, "tb1")
-    for b in range(4):
-        unpack(4 + b, b, "l1", 0, A, ["LQ1"])
-    new_top(1)
-    send_top(2)
-    scores(2, 0, 1)
-    for b in range(4):
-        out_of("A", 4 + b, snd(1), 16, b, A, "ts1")
-    signs(2, 0, 1)
-    cones(2, 2)
-    slots("A", 1, 0)
-    slots("A", 1, 1)
-    bank = {0: 0, 1: 1, 2: 3, 3: 4}
-    for b in range(4):
-        unpack(bank[b], b, "x2", 0, A, top(2))
-        out_of("A", bank[b], own(2), 0, b, A, "tt2")
-    cuts(2, 2)
-    for j in range(5):
-        slot_list(2, j)
-    refill(1, {1: 5, 3: 6, 0: 7, 2: 2})
-    bank = {1: 0, 0: 1, 3: 3, 2: 4}
-    for b in order:
-        unpack(bank[b], b, "l2", 0, A, ["LQ2"])
-    new_bottom(1)
-    low = {0: 5, 1: 6, 2: 7, 3: 2}
-    for b in late:
-        unpack(low[b], b, "x2", A, A, bot(2))
-    tt(T.oab[:, 0:S], ow(2, GP), c0, ALU.subtract, ["gp2", "kv"], ["oa0"])
-    for b in order:
-        out_of(eng_of(b), bank[b], snd(2), 16, b, A, "ts2")
-    slots("A", 2, 1)
-    slots("V", 2, 0)
-    for b in late:
-        out_of("A", low[b], own(2), 2 * A, b, A, "tb2")
-    refill(2, {1: 0, 3: 1, 0: 3, 2: 4})
+    load("ldv", T.vin[:], T.v[:], ["L1"], ["vin"], "dv")
+    quant("v", 0, 128, T.vin[:], ["vin"], "v0")
+    tt("oa0", T.oab[:, 0:S], T.g2[:], T.vv[:, NC - NE::-NE], ALU.subtract, ["g2", "vv"], ["oa0"])
+    ts("oa1", T.oab[:, S:2 * S], T.oab[:, 0:S], 1.0 / GA, None, ALU.mult, None, ["oa0"], ["oa1"])
+    load("stoa", T.oa[:], T.oab[0:128:16, S:2 * S], ["oa1"], [], "stS")
     for h in range(2):
-        parts = (("A", 1, 0, S), ("V", 0, 0, S)) if h == 0 else (("A", 1, 0, S), ("V", 0, 0, CUT2), ("A", 0, CUT2, S))
-        for eng, o, a, b in parts:
-            gather(eng, o, T.xs2[:, 4 * A * h + 32 * a + o:4 * A * h + 32 * b:2], own(2), 6 * A,
-                   T.lf[:, S * h + a:S * h + b], ["lt2", "lx2"], ["tt2", "tb2", "h2"], "x3%d%s" % (h, eng))
-        if h == 0:
-            ts(T.oab[:, S:2 * S], T.oab[:, 0:S], 0.5, None, ALU.mult, None, ["oa0"], ["oa1"])
-            op("S", lambda: g.sync.dma_start(T.oa[:], T.oab[0:128:16, S:2 * S]), ["oa1"], [], "stS")
+        k = str(h)
         quant("x3", A * h, A * h + A, T.xs2[:, 4 * A * h:4 * A * (h + 1)],
-              ["x3%d%s%d" % (h, eng, o) for eng, o, a, b in parts], ["q3%d" % h])
-        mm(5 + h, [("v", 0, "x3", A * h, A)], ["qv", "q3%d" % h])
-        op("S", lambda h=h: g.sync.dma_start(T.oc[:, 4 * A * h:4 * A * (h + 1)],
-                                             T.qx3[:, A * h:A * h + A].bitcast(dt.uint8)), ["q3%d" % h], [], "stS")
-    act(T.yb[:, 0:A], T.ps5[:, 0:A], ACT.Copy, [], ["B5", "yb0"])
-    act(T.yb[:, A:C], T.ps6[:, 0:A], ACT.Copy, [], ["B6", "yb1"])
-    op("A", lambda: SC.dma_start(T.y[:], T.yb[:]), ["yb0", "yb1"], [], "stA")
-    for k in range(4):
-        op("S", lambda k=k: g.sync.dma_start(T.osc[4 * k:4 * k + 4, :], T.sx3[32 * k:32 * k + 4, :]), ["q30", "q31"], [], "stS")
+              gather("end" + k, T.xs2, 4 * A * h, "2", "tbh", T.lf, S * h, ["lt2", "lx2"]), "X" + k)
+        mm("Y" + k, [("v", 0, "x3", A * h, A)], ["v0", "X" + k])
+        load("stc" + k, T.oc[:, 4 * A * h:4 * A * (h + 1)], T.qx3[:, A * h:A * h + A].bitcast(dt.uint8), ["X" + k], [],
+             "stS")
+        out_of("Y" + k, "a", T.yb[:, A * h:A * h + A], 1.0, "yb" + k)
+    op("sty", "A", lambda e: SC.dma_start(T.y[:], T.yb[:]), ["yb0", "yb1"], [], "stA")
+    for j in range(4):
+        load("sts%d" % j, T.osc[4 * j:4 * j + 4, :], T.sx3[32 * j:32 * j + 4, :], ["X0", "X1"], [], "stS")
 
-    _schedule(g, T, [ops[i] for i in ORDER], arrivals, extra)
+    if HOOK:
+        HOOK[0](ops, bank)
+    by_name = {o[0]: o for o in ops}
+    issue = []
+    for word in ORDER.split() or [o[0] for o in ops]:
+        name, eng, fn, r, w, sem = by_name.pop(word.rstrip("*"))
+        if word.endswith("*"):
+            eng = {"a": "v", "v": "a"}[eng]
+        issue.append((name, eng.upper(), fn, r, w, sem))
+    assert not by_name
+    _schedule(g, T, issue, arrivals, extra, bank)

@@ -7,26 +7,54 @@ BF, F32, U16, MXC, MXS = "bfloat16", "float32", "uint16", "float8_e4m3fn_x4", "u
 SMALL = 0.015625
 NE = E + 1
 NC = NE * S
-GA, GC, G0 = 49, 384, 1200
-OWN0, OWN = 54, 1112
-FAR0, FAR = 32, 672
+OWN = 6 * (A + 2 * E)
+FAR0, FAR = 100, 100 + 4 * A
+STEP = 49 / 12
 BIG = 32768.0
 HOOK = []
-CUT = {"x": 13, "top0": 20, "top1": 14, "low0": 12, "low1": 20, "B0": 20, "B1": 20, "B2": 20, "end0": 14, "end1": 8}
+CUT = {"x": 13, "top0": 20, "top1": 12, "low0": 10, "low1": 20, "B0": 20, "B1": 20, "B2": 20, "end0": 20, "end1": 4,
+       "half": 10}
+ORDER = ""
 ORDER = """
-ijp ldx zzb ldu ia2 zb zft qE3 ilu qE0 ip zct ia1 zF0 xtb xta ldwc ldws p2 p8 qT0 pu s2 lu s1 dd1 xb* qu0 ss0 m2 urq urs
-m1 qL0 u48 p16 m3 mQ0 mP0 pq mT00 oQ0 mL00 oP0 ct1 qE1 oT00 ct0 sq0 qE2 mT01 down dd0 mL03 qf0 ivv mT02 qcone oT01 oL00*
-mC0 zH1 mT03 mL01 oC0 mL02 oT03 oT02* fw0 down1 up oL03 bw0 oL01* oL02 sg0 lt0 zF1 gtop0a gtop0b zH0 mF03 qT1 mF01 ra0
-mF00 oF03 mQ1 oF01 mP1 oF00 mF02 oQ1 mT11 oP1 mT13 rb0 oF02* ls0 cown qf1 gB0b gB0a mC1 mT12 mT10 oT13 oC1 oT12* qB0
-oT11 fw1 rc0 oT10* mH01 bw1 rd0 mH00 ls1 sg1 lx0 ra1 oH01 mH02 gB1b* gB1a* mH03 oH02 oH00* oH03* qB1 glow0c glow0b*
-glow0a* sq1 ss1 qL1 rb1 lt1 mL12 mL10 mL11 oL12* mL13 oL10 oL11* oL13 gtop1c* gtop1a* gtop1b* qT2 rc1 mP2 ss2 mQ2 mT21
-sq2 oP2 oQ2 qf2 mC2 mH10 oC2 mH13 mH11 fw2 mH12 bw2 rd1 oH11 mT22 oa0 sg2 lx1 oH13 mT23 oH10 oH12* oa1 oT21 stoa glow1b
-glow1a ldv mF21 mF20 qL2 mF23 oF21* mF22 oF20* mL21 oF23* mL22 oF22* mL23 ls2 mT20 ra2 mL20 gB2b* gB2a* lt2 oL22* rb2
-oT20* qB2 oL20* rc2 oT23 mH21 oL23 rd2 mH23 lx2 oL21* oH21 mH20 oT22 qv0 oH23 mH22 oH20* gend1b* oH22* gend0b gend1c*
-gend0a gend1a* gend0c qX1 qX0 mY1 stc1 stc0 mY0 sts1 sts0 oY1 sts2 sts3 oY0 sty
+z0 ip ldx ldu ia1 zzb1 p8* p16 zzb2 zct3 s1* zzb3* zct1* ia2 p2* m1 u2* k2* zft1* s2* ijp thr mine m2 kap* ivv m3 zF0*
+xtb ldws xta ldwc zb xb* lu qT0 qu0 qE3 sq0 top zft3* ct1 zft2* low* urq urs dd1 ct0 qL0 vv mQ0 zct2* mP0 qE2 qE1 oQ0
+oP0 mL02 qcone mT01 mT03 qf0 oL02* mL03 qE0 dd0 ss0 oT03 mC0 oT01* oL03 mL00 mL01 oC0 mT02 oL00* cown* mT00 oL01 fw0
+oT00* ls0 g0 oT02 lt0 sg0 gtop0b gtop0a zF1* qT1 mQ1 sq1 mP1 ss1 oQ1 oP1 mF01 mF03 mF00 oF01* mF02 oF03 oF00 oF02* qf1
+gB0b ra0 gB0a mC1 mT12 oT12* rb0 qB0 rc0 mH01 rd0 oC1 mH03 lx0 fw1 mH02 oH01* oH03 ls1 mH00 g1 oH02* sg1 mT10 glow0b*
+mF13 oH00* mF12 mF11 mT13 glow0c glow0a mF10 mT11 lt1 oF11 oF12* qL1 oT11 oF10 oT10* ldv mL10 oT13 mL12 mL13 oL10 mL11
+oL12* oL13* oL11 gtop1c gtop1b* gtop1a* oF13 qT2 gB1b gB1a mQ2 ss2 mP2 mT21 sq2 oQ2 oP2 qf2 qv0 qB1 mC2 ra1 mH12 oC2
+mT20 fw2 mT22 rb1 oH12* mH10 ls2 rc1 oT22* mH11 sg2 rd1 oH10 mH13 oH11* mT23 lx1 g2 oH13 oT21 oa0 glow1a glow1b mF23
+mF20 mF22 oF23* mF21 oa1 oF20* oF22 oF21 qL2 gB2a* gB2b* mL21 mL20 mL23 mL22 oL20* ra2 oT23 qB2 oL21 lt2 oL22* rb2 mH21
+oL23 rc2 oT20 mH23 rd2 oH21* mH20 lx2 oa2* oH23 mH22 stoa oH20* gend0b* oH22* gend1b gend0a gend1c gend1a qX0 qX1 stc0*
+mY0 sts1 stc1* mY1 oY0* sts3 oY1* sty0 sty1 sts0* sts2*
 """
-
-SCRATCH = {"xin": ("sbuf", [128, S, 64], BF)}
+ORDER = """
+ldx z0 ip ldu ia2 zft1* p16* p8 dd1 zzb3 s2* p2* ia1 k2* m2 zzb1* zzb2* low s1 top ivv mine zct1 m1 m3 ijp zF1* ldwc xtb
+xta ldws zb thr zct3* xb* qT0 lu qu0 dd0 ss0 qE3 u2 urs urq zct2 zft2* zft3* qE0 ct1 mP0 qE1 mQ0 ct0 oP0 oQ0 qL0 kap
+qcone vv mL03 qf0 mL00 qE2 mT03 sq0 mC0 oL00* mT02 zF0* mL02 oC0 mL01 oT02* cown* mT01 oL02* mT00 fw0 oL03* ls0 oT00* g0
+oL01* oT03 sg0 lt0 oT01 gtop0a gtop0b qT1 mQ1 sq1 mF02 ss1 oQ1 mF03 mF01 oF02* mF00 oF03* mP1 oF01* mT11 oF00* mT12 oP1
+mT10 ra0 gB0b mT13 gB0a oT12* qf1 qB0 mC1 rb0 mH03 rc0 oC1 mH01 rd0 oH03 fw1 mH00 lx0 oH01 ls1 mH02 oH00* sg1 mF10
+glow0b* oH02* glow0a* glow0c* oT13 oT11 qL1 oF10* oT10 g1 mL10 ldv mL12 lt1 mL11 oL10 mL13 oL12* mF12 oL11 mF11 oL13*
+mF13 gtop1a* gtop1b* gtop1c oF12* gB1a* qT2 oF11* ra1 mQ2 ss2 oF13* mP2 sq2 oQ2 oP2 gB1b qf2 mC2 qB1 mT20 mT23 oC2 oT20*
+mH13 fw2 mH11 ls2 mH12 rb1 g2 sg2 mT22 rc1 oa0 mH10 oH12 oa1 rd1 oT22* mT21 oH11* oH13 lx1 qv0 oH10* glow1b* mF20 glow1a*
+mF23 mF22 oT21* mF21 oF23* oF20* oF22 oF21 qL2 gB2a* gB2b* mL22 mL23 mL20 ra2 mL21 qB2 oL21 rb2 oL23 mH23 rc2 oL20* oT23*
+oa2 mH21 lt2 rd2 oL22 oH23 stoa mH20 lx2 oH21 mH22 oH20* gend0b* oH22* gend1b gend0a gend1c gend1a qX0 qX1 mY0 stc0* mY1
+stc1* sts0 oY0* sts2* oY1* sty0* sty1* sts3 sts1
+"""
+ORDER = """
+dd0 ip ldx z0 ldu ia2 zct3* p2 p8 zzb3* zft2* zft3* zct1* u2 ia1 zft1* zzb1 s2* zF0 zct2 s1 m2 p16 zF1 ivv k2 m1 kap thr
+ijp m3 xtb xta ldws ldwc zb zzb2 xb* qT0 qu0 lu qE0 sq0 qE1 urs urq mT00 ct1 qL0 top* oT00* mQ0 qE3 mP0 ct0 low* mL01 qE2
+mL00 mine oQ0 oP0 mT03 mL03 qcone mT01 oL00* qf0 oL03 vv* oL01 oT03 mC0 ss0 mL02 oT01 mT02 oC0 dd1 oT02* oL02* fw0 cown*
+ls0 g0 lt0 sg0 gtop0b gtop0a qT1 mF02 mF00 mF01 mF03 sq1 oF02* mQ1 oF00 mP1 oF01 mT11 ss1 oF03* mT13 oQ1 mT12 ra0 mT10
+oP1 gB0a gB0b qf1 oT11 oT13 qB0 oT12* mC1 rb0 oT10* mH03 rc0 oC1 mH01 rd0 mH00 oH03 fw1 mH02 oH01 lx0 oH00* ls1 mF13 mF11
+oH02* glow0b* mF12 mF10 sg1 glow0c glow0a oF13 g1 oF11 qL1 oF10* lt1 oF12 mL10 ldv mL12 mL13 mL11 oL10* oL12 oL13 oL11*
+gtop1a gtop1c gtop1b gB1a gB1b qT2 ra1 mP2 sq2 rb1 mQ2 mT22 mT21 ss2 oP2 mT20 oQ2 qB1 oT20* qf2 oT22* mH12 rc1 mC2 rd1
+mH11 oH12* mH10 oT21 oC2 mH13 oH11 oH10* fw2 lx1 oH13 ls2 g2 qv0 glow1b glow1a sg2 mF20 mF22 mF23 mF21 oF20* oF22 oa0
+oF21 oF23* qL2 oa1* lt2 mL20 mL22 mL21 mL23 mT23 gB2a* gB2b* ra2 oL21 oL22* qB2 oL23 rb2 oT23 oa2* mH21 rc2 stoa mH23
+rd2 mH20 oH21* mH22 oH23 lx2 oL20 oH20* oH22* gend0b* gend1b gend0a gend1c gend1a qX0 qX1 mY0 stc0 sts1* stc1 mY1 sts0
+oY0* sts2 oY1 sts3 sty0* sty1*
+"""
+SCRATCH = {"xin": ("sbuf", [128, S, 64], BF), "yb": ("sbuf", [128, S, 16], F32)}
 
 
 def _sb(name, n, d):
@@ -40,20 +68,19 @@ def _mx(name, n):
 
 for _n, _w, _d in [("xh", 4 * C, BF), ("uin", 512, BF), ("vin", 512, BF), ("ft", 512, BF), ("ct", 4 * NC, BF),
                    ("zb", 516, BF), ("pf", 16, F32), ("pb", 8, BF), ("jp", 128, BF), ("a1", 216, BF), ("a2", 216, BF),
-                   ("m1", 216, BF), ("m2", 216, BF), ("m3", 216, BF), ("vv", NC, F32), ("cown", S, F32),
-                   ("dd", 2 * S, F32), ("lu0", 8, F32), ("lu", 8, U16), ("yb", C, F32), ("oab", 2 * S, F32),
+                   ("m1", 216, BF), ("m2", 216, BF), ("m3", 216, BF), ("vi", NC, F32), ("vv", NC, F32),
+                   ("cown", S, F32), ("dd", 2 * S, F32), ("z0", NC, BF), ("lu", 8, U16), ("oab", 3 * S, F32),
                    ("lf", 2 * S, U16), ("fa", FAR, BF), ("fb", FAR, BF)]:
     _sb(_n, _w, _d)
-for _n, _w in [("w", 512), ("u", 128), ("ur", 128), ("v", 128), ("c", NC), ("e", 512), ("x3", C), ("o1", A)]:
+for _n, _w in [("w", 512), ("u", 128), ("ur", 128), ("v", 128), ("c", NC), ("e", 512), ("x3", C)]:
     _mx(_n, _w)
 for _t in range(R):
     _mx("x%d" % _t, C)
     _mx("b%d" % _t, A)
     _mx("f%d" % _t, 128)
-    if _t != 1:
-        _mx("l%d" % _t, A)
+    _mx("l%d" % _t, A)
     for _n, _w, _d in [("xs", 4 * C, BF), ("bt", 4 * A, BF), ("wa", OWN, BF), ("wb", OWN, BF), ("d", NC, F32),
-                       ("fw", S, F32), ("g", S, F32), ("rx", 4 * S, F32), ("lnd", S, F32), ("ls", S, U16)]:
+                       ("fw", S, F32), ("g", S, F32), ("rx", 4 * S, F32), ("lnd", S, U16), ("ls", S, U16)]:
         _sb(_n + str(_t), _w, _d)
 for _t in range(R - 1):
     _sb("lt%d" % _t, S, U16)
@@ -61,7 +88,7 @@ for _t in range(R - 1):
 for _b in range(8):
     SCRATCH["ps%d" % _b] = ("psum", [128, 512], F32)
 
-SEMAPHORES = (["cV", "cA", "cP", "cG", "dx", "du", "dw", "dv", "stS", "stA", "gone"]
+SEMAPHORES = (["cV", "cA", "cP", "cG", "dx", "du", "dw", "dv", "st", "gone"]
               + ["rq%d" % t for t in range(R)] + ["rl%d" % t for t in range(R)])
 
 
@@ -129,8 +156,7 @@ def _schedule(g, T, ops, arrivals, extra, bank):
             done[i] = (s, total[s], dict(know[eng]))
     for s in sorted(total):
         if waited.get(s, 0) < total[s]:
-            q = {"stS": g.sync, "stA": g.scalar}.get(s, g)
-            q.wait_ge(T.sem[s], total[s])
+            (g.sync if s == "st" else g).wait_ge(T.sem[s], total[s])
 
 
 def rank_program(g, core, T, topo):
@@ -163,6 +189,9 @@ def rank_program(g, core, T, topo):
     def load(name, out, in_, r, w, sem):
         op(name, "S", lambda e: g.sync.dma_start(out, in_), r, w, sem)
 
+    def store(name, eng, out, in_, r):
+        op(name, eng, lambda e: (g.sync if e == "S" else SC).dma_start(out, in_), r, [], "st")
+
     def ts(name, out, in0, s1, s2, o0, o1, r, w):
         if o1 is None:
             op(name, "V", lambda e: V.tensor_scalar(out, in0, s1, None, o0), r, w)
@@ -172,6 +201,9 @@ def rank_program(g, core, T, topo):
     def tt(name, out, a, b, o, r, w):
         op(name, "V", lambda e: V.tensor_tensor(out, a, b, o), r, w)
 
+    def scan(name, out, a, b, first, o0, o1, r, w):
+        op(name, "V", lambda e: V.tensor_tensor_scan(out, a(), b, first, o0, o1), r, w)
+
     def fill(name, ap, c, w):
         op(name, "V", lambda e: V.memset(ap, c), [], w)
 
@@ -180,6 +212,11 @@ def rank_program(g, core, T, topo):
 
     def act(name, out, in_, func, r, w, **kw):
         op(name, "A", lambda e: SC.activation(out, in_, func, **kw), r, w)
+
+    def affine(name, out, in_, scale, bias, r, w):
+        col = not isinstance(bias, float)
+        op(name, "AV", lambda e: V.tensor_scalar(out, in_, scale, bias, ALU.mult, ALU.add) if e == "V"
+           else SC.activation(out, in_, ACT.Identity if col else ACT.Copy, scale=scale, bias=bias), r, w)
 
     def copy(name, eng, out, in_, r, w):
         op(name, eng, lambda e: V.tensor_copy(out, in_) if e == "V" else SC.activation(out, in_, ACT.Copy), r, w)
@@ -198,16 +235,16 @@ def rank_program(g, core, T, topo):
             return ins
         op("m" + name, "P", fn, r, ["+" + name])
 
-    def out_of(name, eng, dst, scale, w):
+    def out_of(name, eng, dst, scale, w, n=A):
         def fn(e):
-            src = ps(name)[:, 0:A]
+            src = ps(name)[:, 0:n]
             return (V.tensor_scalar(dst, src, scale, None, ALU.mult) if e == "V"
                     else SC.activation(dst, src, ACT.Copy, scale=scale))
         op("o" + name, eng, fn, [], ["-" + name, w])
 
     pf = lambda j: T.pf[:, j:j + 1]
     pb = lambda j: T.pb[:, 2 * j:2 * j + 1]
-    P_, S1, S2, Q_, U_, UP, DOWN, DOWN1, U48 = range(9)
+    P2, S1, S2, K2, U2, KAP, TOP, LOW, THR, MINE = range(10)
     lt = lambda t: T["lt%d" % t][:] if t < R - 1 else T.lf[:, 0:2 * S:2]
     lx = lambda t: T["lx%d" % t][:] if t < R - 1 else T.lf[:, 1:2 * S:2]
 
@@ -222,15 +259,16 @@ def rank_program(g, core, T, topo):
                 first, step = FAR0 + 2 * (b >> 1) + 1, 4
             else:
                 j = "tbh".index(part)
-                first, step = OWN0 + 6 * E * j + 3 * (b >> 1) + j, 6
-            out_of(name + str(b), "av"[1 - (b & 1)], plane(win, b & 1)[:, first:first + step * (A - 1) + 1:step], SMALL,
+                first, step = 6 * E * j + 3 * (b >> 1) + j, 6
+            out_of(name + str(b), ("VA", "AV")[b & 1], plane(win, b & 1)[:, first:first + step * (A - 1) + 1:step], SMALL,
                    win + part + str(b))
 
-    def gather(name, tile, first, win, parts, lst, col, r):
+    def gather(name, tile, first, win, parts, lst, col, r, n=S):
         made = []
-        for piece, eng, o, a, b in (("b", "a", 1, 0, S), ("a", "v", 0, 0, CUT[name]), ("c", "a", 0, CUT[name], S)):
+        for piece, eng, o, a, b in (("b", "AV", 1, 0, n), ("a", "VA", 0, 0, CUT[name]), ("c", "AV", 0, CUT[name], n)):
             if a < b:
-                keys = [("" if p in parts else "?") + win + p + str(j) for p in "tbhz" for j in (o, o + 2)]
+                keys = [("" if p in parts else "?") + win + p + str(j) for p in ("tz" if win == "F" else "tbh")
+                        for j in (o, o + 2)]
                 copy("g" + name + piece, eng, tile[:, first + 32 * a + o:first + 32 * b:2],
                      plane(win, o)[:].indirect(lst[:, col + a:col + b]), r + keys, [name + piece])
                 made.append(name + piece)
@@ -241,100 +279,97 @@ def rank_program(g, core, T, topo):
     load("ldwc", T.qw[:].bitcast(dt.uint8), T.wc[:], ["xin"], ["qw"], "dw")
     load("ldws", T.sw[:], T.ws[:], ["xin"], ["sw"], "dw")
 
-    iota("ip", pf(P_), [[0, 1]], 0, 1, ["p"])
+    base = round(24 * (FAR0 - STEP * (1 + 1120) + 640) + 13)
+    iota("ip", pf(P2), [[0, 1]], 0, 2, ["p"])
     iota("ia1", T.a1[:], [[1, 24], [1, NE]], -S, -1, ["a1"])
     iota("ia2", T.a2[:], [[-1, 24], [1, NE]], S - 2, -1, ["a2"])
-    iota("ilu", T.lu0[:], [[16, 8]], 0, 0, ["lu0"])
     iota("ijp", T.jp[:], [[1, 128]], 0, -1, ["jp"])
-    iota("ivv", T.vv[:], [[-GC, S], [GA, NE]], G0 + GC * (S - 1), 0, ["vv"])
-    fill("zct", T.ct[:], 0.0, ["ct0", "ct1"])
-    fill("zft", T.ft[:], 0.0, ["ft"])
-    fill("zzb", T.zb[:], 0.0, ["zb"])
-    fill("dd0", T.dd[:, 0:S], float(-GC - GA), ["dd0"])
-    fill("dd1", T.dd[:, S:2 * S], float(GC - GA), ["dd1"])
-    act("p8", pb(0), pf(P_), ACT.Copy, ["p"], ["p8"], bias=1280 - 3.5)
-    act("p16", pb(1), pf(P_), ACT.Copy, ["p"], ["p16"], bias=2560 - 7.5)
-    act("p2", pb(2), pf(P_), ACT.Copy, ["p"], ["p2"], bias=320 - 0.5)
-    act("s1", pf(S1), pb(0), ACT.Copy, ["p8"], ["s1"], scale=-1.125, bias=1440.0)
-    act("s2", pf(S2), pb(0), ACT.Copy, ["p8"], ["s2"], scale=-0.875, bias=1120.0)
-    act("pq", pf(Q_), pb(1), ACT.Identity, ["p16", "p"], ["q"], scale=-1.0, bias=pf(P_))
-    act("pu", pf(U_), pb(2), ACT.Identity, ["p2", "p"], ["u"], scale=-1.0, bias=pf(P_))
-    act("up", pf(UP), pf(Q_), ACT.Copy, ["q"], ["up"], scale=24.5, bias=24.5 * 2560 - 3.75 - G0 + E * OWN0)
-    act("u48", pf(U48), pf(U_), ACT.Copy, ["u"], ["u48"], scale=48.5,
-        bias=48.5 * 320 - 24.5 * 2560 - G0 - GA + 12 * FAR0 + 6.5)
-    act("down", pf(DOWN), pf(Q_), ACT.Identity, ["q", "u48"], ["down"], scale=-24.5, bias=pf(U48))
-    act("down1", pf(DOWN1), pf(DOWN), ACT.Copy, ["down"], ["down1"], bias=E * OWN0 - 3.5 - 12 * FAR0 - 6.5)
-    act("cown", T.cown[:], T.vv[:, NC - 1::-NE], ACT.Identity, ["vv", "down1"], ["cown"], bias=pf(DOWN1))
+    iota("ivv", T.vi[:], [[-768, S], [98, NE]], base + 768 * (S - 1), 0, ["vi"])
+    fill("z0", T.z0[:], 0.0, ["z0"])
+    for j in (1, 2, 3):
+        for name, ap, n in (("ct", T.ct[:, j:4 * NC:4], NC), ("ft", T.ft[:, j:512:4], 128),
+                            ("zb", T.zb[:, j - 1:516:4], 129)):
+            op("z%s%d" % (name, j), "AV", lambda e, ap=ap, n=n: V.memset(ap, 0.0) if e == "V"
+               else SC.activation(ap, T.z0[:, 0:n], ACT.Copy), ["z0"], ["%s%d" % (name, j)])
+    for o in (0, 1):
+        ap = plane("F", o)[:, FAR0 - 4 * E:FAR0 - 4 * E + 4 * A:2]
+        op("zF%d" % o, "VG", lambda e, ap=ap: V.memset(ap, 0.0) if e == "V"
+           else g.iota(ap, [[0, 2 * A]], 0, 0, allow_small_or_imprecise_dtypes=True), [], ["Fz%d" % o, "Fz%d" % (o + 2)])
+    fill("dd0", T.dd[:, 0:S], -32 - STEP, ["dd0"])
+    fill("dd1", T.dd[:, S:2 * S], 32 - STEP, ["dd1"])
+    affine("p8", pb(0), pf(P2), 0.5, 1280 - 3.5, ["p"], ["p8"])
+    affine("p16", pb(1), pf(P2), 0.5, 2560 - 7.5, ["p"], ["p16"])
+    affine("p2", pb(2), pf(P2), 0.5, 320 - 0.5, ["p"], ["p2"])
+    affine("s1", pf(S1), pb(0), -1.125, 1440.0, ["p8"], ["s1"])
+    affine("s2", pf(S2), pb(0), -0.875, 1120.0, ["p8"], ["s2"])
+    affine("k2", pf(K2), pb(1), -1.0, pb(2), ["p16", "p2"], ["k2"])
+    affine("u2", pf(U2), pb(2), -2.0, pf(P2), ["p2", "p"], ["u2"])
+    affine("kap", pf(KAP), pf(K2), -STEP / 2, pf(U2), ["k2", "u2"], ["kap"])
+    affine("vv", T.vv[:], T.vi[:], 1 / 24, pf(KAP), ["vi", "kap"], ["vv"])
+    first = 6.125 * (1 + 2240) - 0.4375 - 1.5 * (FAR0 + 13 / 24)
+    affine("top", pf(TOP), pf(K2), 6.125, first, ["k2"], ["top"])
+    affine("low", pf(LOW), pf(K2), 6.125, first + 49, ["k2"], ["low"])
+    affine("thr", pf(THR), pf(K2), -2.0, 30.0 - 2 * 2240, ["k2"], ["thr"])
+    affine("mine", pf(MINE), pf(K2), -STEP, -STEP * (1 + 2240), ["k2"], ["mine"])
+    affine("cown", T.cown[:], T.vv[:, NC - NE::-NE], 1.0, pf(MINE), ["vv", "mine"], ["cown"])
     ts("m1", T.m1[:], T.a1[:], pf(S1), BIG, ALU.is_ge, ALU.mult, ["a1", "s1"], ["m1"])
     ts("m2", T.m2[:], T.a2[:], pf(S2), None, ALU.is_ge, None, ["a2", "s2"], ["m2"])
     tt("m3", T.m3[:], T.m1[:], T.m2[:], ALU.mult, ["m1", "m2"], ["m3"])
-    act("ct0", T.ct[:, 0:4 * NC:4], T.m3[:, 0:NC], ACT.Copy, ["m3"], ["ct0"])
-    act("ct1", T.ct[96:128, 1:4 * NC:4], T.m3[96:128, 4 * NE:4 * NE + NC], ACT.Copy, ["m3"], ["ct1"], scale=0.5)
-    quant("c", 0, NC, T.ct[:], ["ct0", "ct1"], "cone")
-    copy("lu", "V", T.lu[:], T.lu0[:], ["lu0"], ["lu"])
-    ts("zb", T.zb[:, 3:515:4], T.jp[:], 0.0, 64.0, ALU.is_equal, ALU.mult, ["jp"], ["zb"])
+    affine("ct0", T.ct[:, 0:4 * NC:4], T.m3[:, 0:NC], 1.0, 0.0, ["m3"], ["ct0"])
+    affine("ct1", T.ct[96:128, 1:4 * NC:4], T.m3[96:128, 4 * NE:4 * NE + NC], 0.5, 0.0, ["m3"], ["ct1"])
+    quant("c", 0, NC, T.ct[:], ["ct0", "ct1", "ct2", "ct3"], "cone")
+    ts("lu", T.lu[:], T.vi[:, NC - NE:NC - NE - 8 * NE:-NE], float(-base), 16 / 768, ALU.add, ALU.mult, ["vi"], ["lu"])
+    ts("zb", T.zb[:, 3:515:4], T.jp[:], 0.0, 64.0, ALU.is_equal, ALU.mult, ["jp"], ["zb0"])
     for b in range(4):
-        quant("e", 128 * b, 128 * b + 128, T.zb[:, 3 - b:515 - b], ["zb"], "E%d" % b)
-    for o in (0, 1):
-        iota("zF%d" % o, plane("F", o)[:, 0:4 * A:2], [[0, 2 * A]], 0, 0, ["Fz%d" % o, "Fz%d" % (o + 2)])
-        iota("zH%d" % o, plane("1", o)[:, 5:963:3], [[0, 2 * A]], 0, 0, ["1h%d" % o, "1h%d" % (o + 2)])
+        quant("e", 128 * b, 128 * b + 128, T.zb[:, 3 - b:515 - b], ["zb0", "zb1", "zb2", "zb3"], "E%d" % b)
 
-    copy("xtb", "a", T.xh[:, 32 * CUT["x"]:4 * A], T.xin[:, CUT["x"]:S, 0:32], ["xin"], ["xtb"])
-    copy("xta", "v", T.xh[:, 0:32 * CUT["x"]], T.xin[:, 0:CUT["x"], 0:32], ["xin"], ["xta"])
+    copy("xtb", "AV", T.xh[:, 32 * CUT["x"]:4 * A], T.xin[:, CUT["x"]:S, 0:32], ["xin"], ["xtb"])
+    copy("xta", "VA", T.xh[:, 0:32 * CUT["x"]], T.xin[:, 0:CUT["x"], 0:32], ["xin"], ["xta"])
     quant("x0", 0, A, T.xh[:, 0:4 * A], ["xta", "xtb"], "T0")
-    copy("xb", "v", T.xh[:, 4 * A:8 * A], T.xin[:, :, 32:64], ["xin"], ["xb"])
+    copy("xb", "VA", T.xh[:, 4 * A:8 * A], T.xin[:, :, 32:64], ["xin"], ["xb"])
     quant("x0", A, C, T.xh[:, 4 * A:8 * A], ["xb"], "L0")
     quant("u", 0, 128, T.uin[:], ["uin"], "u0")
     op("urq", "V", lambda e: V.tensor_copy(T.qur[:].bitcast(dt.uint32), T.qu[:].bitcast(dt.uint32).indirect(T.lu[:])),
        ["u0", "lu"], ["qur"])
-    copy("urs", "a", T.sur[:], T.su[:].indirect(T.lu[:]), ["u0", "lu"], ["sur"])
+    copy("urs", "AV", T.sur[:], T.su[:].indirect(T.lu[:]), ["u0", "lu"], ["sur"])
 
     for t in range(R):
-        k = str(t)
+        k, n = str(t), str(t + 1)
         x, gg, lnd = "x" + k, T["g" + k], T["lnd" + k]
         rx = lambda i: T["rx" + k][:, S * i:S * i + S]
-        if t != 1:
-            send("sq" + k, t, T["ql" + k][:].bitcast(dt.uint8), T["q" + x][:, 0:A].bitcast(dt.uint8), "rq" + k, ["T" + k])
-            send("ss" + k, t, T["sl" + k][:], T["s" + x][:, 0:A], "rq" + k, ["T" + k])
+        send("sq" + k, t, T["ql" + k][:].bitcast(dt.uint8), T["q" + x][:, 0:A].bitcast(dt.uint8), "rq" + k, ["T" + k])
+        send("ss" + k, t, T["sl" + k][:], T["s" + x][:, 0:A], "rq" + k, ["T" + k])
         mm("P" + k, [(x, 0, "ur", 0, 128)], ["T" + k, "qur", "sur"])
         mm("Q" + k, [(x, 32, "ur", 0, 128)], ["T" + k, "qur", "sur"])
         op("oP" + k, "V", lambda e, k=k: V.tensor_scalar(T.ft[:, 0:512:4], ps("P" + k)[:, 0:128], 0.0, 0.5, ALU.is_gt,
-                                                         ALU.subtract), ["ft"], ["-P" + k, "ft0"])
+                                                         ALU.subtract), [], ["-P" + k, "ft0"])
         op("oQ" + k, "A", lambda e, k=k: SC.activation(T.ft[96:128, 1:512:4], ps("Q" + k)[96:128, 0:128], ACT.Sign,
-                                                       bias=-2.0 ** -126), ["ft"], ["-Q" + k, "ft1"])
-        quant("f" + k, 0, 128, T.ft[:], ["ft0", "ft1"], "f" + k)
+                                                       bias=-2.0 ** -126), [], ["-Q" + k, "ft1"])
+        quant("f" + k, 0, 128, T.ft[:], ["ft0", "ft1", "ft2", "ft3"], "f" + k)
         mm("C" + k, [("f" + k, 0, "c", 0, NC)], ["f" + k, "cone"])
-        op("oC" + k, "V", lambda e, k=k: V.tensor_tensor_scan(T["d" + k][:], ps("C" + k)[:, 0:NC], T.vv[:], BIG, ALU.max,
-                                                              ALU.min), ["vv"], ["-C" + k, "d" + k])
-        op("fw" + k, "V", lambda e, k=k: V.tensor_tensor_scan(T["fw" + k][:], T.dd[:, 0:S], T["d" + k][:, E:NC:NE], 0.0,
-                                                              ALU.add, ALU.max), ["dd0", "d" + k], ["fw" + k])
-        op("bw" + k, "V", lambda e, k=k: V.tensor_tensor_scan(T["g" + k][:], T.dd[:, S:2 * S], T["fw" + k][:, S - 1::-1],
-                                                              -BIG, ALU.add, ALU.max), ["dd1", "fw" + k], ["g" + k])
-        send("sg" + k, t, lnd[:], gg[:], "rl" + k, ["g" + k])
+        scan("oC" + k, T["d" + k][:], lambda k=k: ps("C" + k)[:, 0:NC], T.vv[:], BIG, ALU.max, ALU.min, ["vv"],
+             ["-C" + k, "d" + k])
+        scan("fw" + k, T["fw" + k][:], lambda: T.dd[:, 0:S], T["d" + k][:, E:NC:NE], 0.0, ALU.add, ALU.max,
+             ["dd0", "d" + k], ["fw" + k])
+        for name, out in (("ls" + k, T["ls" + k]), ("g" + k, gg)):
+            scan(name, out[:], lambda: T.dd[:, S:2 * S], T["fw" + k][:, S - 1::-1], -BIG, ALU.add, ALU.max,
+                 ["dd1", "fw" + k], [name])
+        send("sg" + k, t, lnd[:], T["ls" + k][:], "rl" + k, ["ls" + k])
         product("T" + k, k, "t", lambda b: [("e", 128 * b, x, 0, A)], ["T" + k])
-        if t == 1:
-            ts("ls1", T.ls1[:], gg[:], pf(DOWN1), 0.125, ALU.add, ALU.mult, ["g1", "down1"], ["ls1"])
-            quant("o1", 0, A, T.bt1[:], gather("B1", T.bt1, 0, "1", "th", T.ls1, 0, ["ls1"]), "B1")
-            send("sq1", t, T.qb1[:].bitcast(dt.uint8), T.qo1[:].bitcast(dt.uint8), "rq1", ["B1"])
-            send("ss1", t, T.sb1[:], T.so1[:], "rq1", ["B1"])
-        else:
-            product("F" + k, "F", "t", lambda b: [("e", 128 * b, "l" + k, 0, A)], ["LQ" + k])
-            ts("ls" + k, T["ls" + k][:], lnd[:], pf(DOWN), 1.0 / 12, ALU.add, ALU.mult, ["LL" + k, "down"], ["ls" + k])
-            quant("b" + k, 0, A, T["bt" + k][:], gather("B" + k, T["bt" + k], 0, "F", "tz", T["ls" + k], 0, ["ls" + k]),
-                  "B" + k)
+        product("F" + k, "F", "t", lambda b: [("e", 128 * b, "l" + k, 0, A)], ["LQ" + k])
+        quant("b" + k, 0, A, T["bt" + k][:], gather("B" + k, T["bt" + k], 0, "F", "tz", lnd, 0, ["LL" + k]), "B" + k)
         product("L" + k, k, "b", lambda b: [("e", 128 * b, x, A, A)], ["L" + k])
-        ts("lt" + k, lt(t), gg[:], pf(UP), 0.125, ALU.add, ALU.mult, ["g" + k, "up"], ["lt" + k])
-        ts("ra" + k, rx(0), gg[:], pf(UP), float(GA * E), ALU.add, ALU.add, ["g" + k, "up"], ["ra" + k])
-        tt("rb" + k, rx(1), lnd[:], rx(0), ALU.is_gt, ["LL" + k, "ra" + k], ["rb" + k])
-        tt("rc" + k, rx(2), rx(1), rx(0), ALU.mult, ["rb" + k, "ra" + k], ["rc" + k])
+        ts("lt" + k, lt(t), gg[:], 1.5, pf(TOP), ALU.mult, ALU.add, ["g" + k, "top"], ["lt" + k])
+        ts("ra" + k, rx(0), lnd[:], pf(THR), None, ALU.add, None, ["LL" + k, "thr"], ["ra" + k])
+        tt("rb" + k, rx(1), rx(0), gg[:], ALU.is_gt, ["g" + k, "ra" + k], ["rb" + k])
+        tt("rc" + k, rx(2), rx(1), gg[:], ALU.mult, ["rb" + k, "g" + k], ["rc" + k])
         tt("rd" + k, rx(3), rx(2), T.cown[:], ALU.max, ["rc" + k, "cown"], ["rd" + k])
-        ts("lx" + k, lx(t), rx(3), 0.125, None, ALU.mult, None, ["rd" + k], ["lx" + k])
+        ts("lx" + k, lx(t), rx(3), 1.5, pf(LOW), ALU.mult, ALU.add, ["rd" + k, "low"], ["lx" + k])
         if t < R - 1:
-            n = str(t + 1)
             quant("x" + n, 0, A, T["xs" + k][:, 0:4 * A],
                   gather("top" + k, T["xs" + k], 0, k, "tb", T["lt" + k], 0, ["lt" + k]), "T" + n)
         product("H" + k, k, "h", lambda b: [("w", 128 * b, "b" + k, 0, A), ("e", 128 * b, "b" + k, 0, A)],
-                ["LQ1" if t == 1 else "B" + k, "qw", "sw"])
+                ["B" + k, "qw", "sw"])
         if t < R - 1:
             quant("x" + n, A, C, T["xs" + k][:, 4 * A:8 * A],
                   gather("low" + k, T["xs" + k], 4 * A, k, "tbh", T["lx" + k], 0, ["lx" + k]), "L" + n)
@@ -342,19 +377,19 @@ def rank_program(g, core, T, topo):
     load("ldv", T.vin[:], T.v[:], ["L1"], ["vin"], "dv")
     quant("v", 0, 128, T.vin[:], ["vin"], "v0")
     tt("oa0", T.oab[:, 0:S], T.g2[:], T.vv[:, NC - NE::-NE], ALU.subtract, ["g2", "vv"], ["oa0"])
-    ts("oa1", T.oab[:, S:2 * S], T.oab[:, 0:S], 1.0 / GA, None, ALU.mult, None, ["oa0"], ["oa1"])
-    load("stoa", T.oa[:], T.oab[0:128:16, S:2 * S], ["oa1"], [], "stS")
-    for h in range(2):
+    affine("oa1", T.oab[:, S:2 * S], T.oab[:, 0:S], 1 / STEP, 2.0 ** 23, ["oa0"], ["oa1"])
+    affine("oa2", T.oab[:, 2 * S:3 * S], T.oab[:, S:2 * S], 1.0, -2.0 ** 23, ["oa1"], ["oa2"])
+    store("stoa", "SA", T.oa[:], T.oab[0:128:16, 2 * S:3 * S], ["oa2"])
+    for h, (a, b) in enumerate(((0, CUT["half"]), (CUT["half"], S))):
         k = str(h)
-        quant("x3", A * h, A * h + A, T.xs2[:, 4 * A * h:4 * A * (h + 1)],
-              gather("end" + k, T.xs2, 4 * A * h, "2", "tbh", T.lf, S * h, ["lt2", "lx2"]), "X" + k)
-        mm("Y" + k, [("v", 0, "x3", A * h, A)], ["v0", "X" + k])
-        load("stc" + k, T.oc[:, 4 * A * h:4 * A * (h + 1)], T.qx3[:, A * h:A * h + A].bitcast(dt.uint8), ["X" + k], [],
-             "stS")
-        out_of("Y" + k, "a", T.yb[:, A * h:A * h + A], 1.0, "yb" + k)
-    op("sty", "A", lambda e: SC.dma_start(T.y[:], T.yb[:]), ["yb0", "yb1"], [], "stA")
+        quant("x3", 16 * a, 16 * b, T.xs2[:, 64 * a:64 * b],
+              gather("end" + k, T.xs2, 64 * a, "2", "tbh", T.lf, 2 * a, ["lt2", "lx2"], 2 * (b - a)), "X" + k)
+        mm("Y" + k, [("v", 0, "x3", 16 * a, 16 * (b - a))], ["v0", "X" + k])
+        store("stc" + k, "SA", T.oc[:, 64 * a:64 * b], T.qx3[:, 16 * a:16 * b].bitcast(dt.uint8), ["X" + k])
+        out_of("Y" + k, "AV", T.yb[:, a:b, :], 1.0, "yb" + k, 16 * (b - a))
+        store("sty" + k, "AS", T.y[:, 16 * a:16 * b], T.yb[:, a:b, :], ["yb" + k])
     for j in range(4):
-        load("sts%d" % j, T.osc[4 * j:4 * j + 4, :], T.sx3[32 * j:32 * j + 4, :], ["X0", "X1"], [], "stS")
+        store("sts%d" % j, "SA", T.osc[4 * j:4 * j + 4, :], T.sx3[32 * j:32 * j + 4, :], ["X0", "X1"])
 
     if HOOK:
         HOOK[0](ops, bank)
@@ -362,8 +397,6 @@ def rank_program(g, core, T, topo):
     issue = []
     for word in ORDER.split() or [o[0] for o in ops]:
         name, eng, fn, r, w, sem = by_name.pop(word.rstrip("*"))
-        if word.endswith("*"):
-            eng = {"a": "v", "v": "a"}[eng]
-        issue.append((name, eng.upper(), fn, r, w, sem))
+        issue.append((name, eng[word.endswith("*")], fn, r, w, sem))
     assert not by_name
     _schedule(g, T, issue, arrivals, extra, bank)

from concourse.mybir import dt, AluOpType, ActivationFunctionType

ALU = AluOpType
ACT = ActivationFunctionType
S, E, A, C, R = 20, 8, 160, 320, 3
BF, F32, U16, MXC, MXS = "bfloat16", "float32", "uint16", "float8_e4m3fn_x4", "uint8"
SMALL = 0.015625
NE = E + 1
NC = NE * S
OWN = 6 * (A + 2 * E)
FAR0, FAR = 100, 100 + 4 * A
STEP = 49 / 12
BIG = 32768.0
HOOK = []
CUT = {"x": 13, "top0": 20, "top1": 12, "low0": 10, "low1": 20, "B0": 20, "B1": 20, "B2": 20, "end0": 20, "end1": 4,
       "half": 10}
ORDER = ""
ORDER = """
z0 ip ldx ldu ia1 zzb1 p8* p16 zzb2 zct3 s1* zzb3* zct1* ia2 p2* m1 u2* k2* zft1* s2* ijp thr mine m2 kap* ivv m3 zF0*
xtb ldws xta ldwc zb xb* lu qT0 qu0 qE3 sq0 top zft3* ct1 zft2* low* urq urs dd1 ct0 qL0 vv mQ0 zct2* mP0 qE2 qE1 oQ0
oP0 mL02 qcone mT01 mT03 qf0 oL02* mL03 qE0 dd0 ss0 oT03 mC0 oT01* oL03 mL00 mL01 oC0 mT02 oL00* cown* mT00 oL01 fw0
oT00* ls0 g0 oT02 lt0 sg0 gtop0b gtop0a zF1* qT1 mQ1 sq1 mP1 ss1 oQ1 oP1 mF01 mF03 mF00 oF01* mF02 oF03 oF00 oF02* qf1
gB0b ra0 gB0a mC1 mT12 oT12* rb0 qB0 rc0 mH01 rd0 oC1 mH03 lx0 fw1 mH02 oH01* oH03 ls1 mH00 g1 oH02* sg1 mT10 glow0b*
mF13 oH00* mF12 mF11 mT13 glow0c glow0a mF10 mT11 lt1 oF11 oF12* qL1 oT11 oF10 oT10* ldv mL10 oT13 mL12 mL13 oL10 mL11
oL12* oL13* oL11 gtop1c gtop1b* gtop1a* oF13 qT2 gB1b gB1a mQ2 ss2 mP2 mT21 sq2 oQ2 oP2 qf2 qv0 qB1 mC2 ra1 mH12 oC2
mT20 fw2 mT22 rb1 oH12* mH10 ls2 rc1 oT22* mH11 sg2 rd1 oH10 mH13 oH11* mT23 lx1 g2 oH13 oT21 oa0 glow1a glow1b mF23
mF20 mF22 oF23* mF21 oa1 oF20* oF22 oF21 qL2 gB2a* gB2b* mL21 mL20 mL23 mL22 oL20* ra2 oT23 qB2 oL21 lt2 oL22* rb2 mH21
oL23 rc2 oT20 mH23 rd2 oH21* mH20 lx2 oa2* oH23 mH22 stoa oH20* gend0b* oH22* gend1b gend0a gend1c gend1a qX0 qX1 stc0*
mY0 sts1 stc1* mY1 oY0* sts3 oY1* sty0 sty1 sts0* sts2*
"""
ORDER = """
ldx z0 ip ldu ia2 zft1* p16* p8 dd1 zzb3 s2* p2* ia1 k2* m2 zzb1* zzb2* low s1 top ivv mine zct1 m1 m3 ijp zF1* ldwc xtb
xta ldws zb thr zct3* xb* qT0 lu qu0 dd0 ss0 qE3 u2 urs urq zct2 zft2* zft3* qE0 ct1 mP0 qE1 mQ0 ct0 oP0 oQ0 qL0 kap
qcone vv mL03 qf0 mL00 qE2 mT03 sq0 mC0 oL00* mT02 zF0* mL02 oC0 mL01 oT02* cown* mT01 oL02* mT00 fw0 oL03* ls0 oT00* g0
oL01* oT03 sg0 lt0 oT01 gtop0a gtop0b qT1 mQ1 sq1 mF02 ss1 oQ1 mF03 mF01 oF02* mF00 oF03* mP1 oF01* mT11 oF00* mT12 oP1
mT10 ra0 gB0b mT13 gB0a oT12* qf1 qB0 mC1 rb0 mH03 rc0 oC1 mH01 rd0 oH03 fw1 mH00 lx0 oH01 ls1 mH02 oH00* sg1 mF10
glow0b* oH02* glow0a* glow0c* oT13 oT11 qL1 oF10* oT10 g1 mL10 ldv mL12 lt1 mL11 oL10 mL13 oL12* mF12 oL11 mF11 oL13*
mF13 gtop1a* gtop1b* gtop1c oF12* gB1a* qT2 oF11* ra1 mQ2 ss2 oF13* mP2 sq2 oQ2 oP2 gB1b qf2 mC2 qB1 mT20 mT23 oC2 oT20*
mH13 fw2 mH11 ls2 mH12 rb1 g2 sg2 mT22 rc1 oa0 mH10 oH12 oa1 rd1 oT22* mT21 oH11* oH13 lx1 qv0 oH10* glow1b* mF20 glow1a*
mF23 mF22 oT21* mF21 oF23* oF20* oF22 oF21 qL2 gB2a* gB2b* mL22 mL23 mL20 ra2 mL21 qB2 oL21 rb2 oL23 mH23 rc2 oL20* oT23*
oa2 mH21 lt2 rd2 oL22 oH23 stoa mH20 lx2 oH21 mH22 oH20* gend0b* oH22* gend1b gend0a gend1c gend1a qX0 qX1 mY0 stc0* mY1
stc1* sts0 oY0* sts2* oY1* sty0* sty1* sts3 sts1
"""
ORDER = """
dd0 ip ldx z0 ldu ia2 zct3* p2 p8 zzb3* zft2* zft3* zct1* u2 ia1 zft1* zzb1 s2* zF0 zct2 s1 m2 p16 zF1 ivv k2 m1 kap thr
ijp m3 xtb xta ldws ldwc zb zzb2 xb* qT0 qu0 lu qE0 sq0 qE1 urs urq mT00 ct1 qL0 top* oT00* mQ0 qE3 mP0 ct0 low* mL01 qE2
mL00 mine oQ0 oP0 mT03 mL03 qcone mT01 oL00* qf0 oL03 vv* oL01 oT03 mC0 ss0 mL02 oT01 mT02 oC0 dd1 oT02* oL02* fw0 cown*
ls0 g0 lt0 sg0 gtop0b gtop0a qT1 mF02 mF00 mF01 mF03 sq1 oF02* mQ1 oF00 mP1 oF01 mT11 ss1 oF03* mT13 oQ1 mT12 ra0 mT10
oP1 gB0a gB0b qf1 oT11 oT13 qB0 oT12* mC1 rb0 oT10* mH03 rc0 oC1 mH01 rd0 mH00 oH03 fw1 mH02 oH01 lx0 oH00* ls1 mF13 mF11
oH02* glow0b* mF12 mF10 sg1 glow0c glow0a oF13 g1 oF11 qL1 oF10* lt1 oF12 mL10 ldv mL12 mL13 mL11 oL10* oL12 oL13 oL11*
gtop1a gtop1c gtop1b gB1a gB1b qT2 ra1 mP2 sq2 rb1 mQ2 mT22 mT21 ss2 oP2 mT20 oQ2 qB1 oT20* qf2 oT22* mH12 rc1 mC2 rd1
mH11 oH12* mH10 oT21 oC2 mH13 oH11 oH10* fw2 lx1 oH13 ls2 g2 qv0 glow1b glow1a sg2 mF20 mF22 mF23 mF21 oF20* oF22 oa0
oF21 oF23* qL2 oa1* lt2 mL20 mL22 mL21 mL23 mT23 gB2a* gB2b* ra2 oL21 oL22* qB2 oL23 rb2 oT23 oa2* mH21 rc2 stoa mH23
rd2 mH20 oH21* mH22 oH23 lx2 oL20 oH20* oH22* gend0b* gend1b gend0a gend1c gend1a qX0 qX1 mY0 stc0 sts1* stc1 mY1 sts0
oY0* sts2 oY1 sts3 sty0* sty1*
"""
SCRATCH = {"xin": ("sbuf", [128, S, 64], BF), "yb": ("sbuf", [128, S, 16], F32)}


def _sb(name, n, d):
    SCRATCH[name] = ("sbuf", [128, n], d)


def _mx(name, n):
    _sb("q" + name, n, MXC)
    _sb("s" + name, n, MXS)


for _n, _w, _d in [("xh", 4 * C, BF), ("uin", 512, BF), ("vin", 512, BF), ("ft", 512, BF), ("ct", 4 * NC, BF),
                   ("zb", 516, BF), ("pf", 16, F32), ("pb", 8, BF), ("jp", 128, BF), ("a1", 216, BF), ("a2", 216, BF),
                   ("m1", 216, BF), ("m2", 216, BF), ("m3", 216, BF), ("vi", NC, F32), ("vv", NC, F32),
                   ("cown", S, F32), ("dd", 2 * S, F32), ("z0", NC, BF), ("lu", 8, U16), ("oab", 3 * S, F32),
                   ("lf", 2 * S, U16), ("fa", FAR, BF), ("fb", FAR, BF)]:
    _sb(_n, _w, _d)
for _n, _w in [("w", 512), ("u", 128), ("ur", 128), ("v", 128), ("c", NC), ("e", 512), ("x3", C)]:
    _mx(_n, _w)
for _t in range(R):
    _mx("x%d" % _t, C)
    _mx("b%d" % _t, A)
    _mx("f%d" % _t, 128)
    _mx("l%d" % _t, A)
    for _n, _w, _d in [("xs", 4 * C, BF), ("bt", 4 * A, BF), ("wa", OWN, BF), ("wb", OWN, BF), ("d", NC, F32),
                       ("fw", S, F32), ("g", S, F32), ("rx", 4 * S, F32), ("lnd", S, U16), ("ls", S, U16)]:
        _sb(_n + str(_t), _w, _d)
for _t in range(R - 1):
    _sb("lt%d" % _t, S, U16)
    _sb("lx%d" % _t, S, U16)
for _b in range(8):
    SCRATCH["ps%d" % _b] = ("psum", [128, 512], F32)

SEMAPHORES = (["cV", "cA", "cP", "cG", "dx", "du", "dw", "dv", "st", "gone"]
              + ["rq%d" % t for t in range(R)] + ["rl%d" % t for t in range(R)])


def _schedule(g, T, ops, arrivals, extra, bank):
    queue = {"V": g.vector, "A": g.scalar, "P": g.tensor, "G": g, "S": g.sync}
    writer, readers, deps = dict(arrivals), {}, []
    marked = set()
    free = list(range(8))
    for i, (name, eng, fn, r, w, sem) in enumerate(ops):
        w = list(w)
        for k in list(w):
            if k[0] in "+-":
                if k[0] == "+":
                    bank[k[1:]] = free.pop(0)
                else:
                    free.append(bank[k[1:]])
                w[w.index(k)] = "bank%d" % bank[k[1:]]
        d = []
        for k in r:
            if k[0] != "?":
                d.append(writer[k])
            elif k[1:] in writer:
                d.append(writer[k[1:]])
        for k in w:
            if k in writer:
                d.append(writer[k])
            d.extend(readers.get(k, []))
        d = [x for x in d if x != i]
        deps.append(d)
        for x in d:
            if isinstance(x, int):
                marked.add(x)
        for k in r:
            readers.setdefault(k.lstrip("?"), []).append(i)
        for k in w:
            writer[k] = i
            readers[k] = []
    total = dict(extra)
    shared = {}
    for name, eng, fn, r, w, sem in ops:
        if sem is not None:
            shared[sem] = shared.get(sem, 0) + 16
    know = {e: {} for e in queue}
    done, waited = {}, {}
    for i, (name, eng, fn, r, w, sem) in enumerate(ops):
        local = sorted(set(x for x in deps[i] if isinstance(x, int)), reverse=True)
        need = [done[x] for x in local] + [(x[0], x[1], {}) for x in deps[i] if not isinstance(x, int)]
        for s, v, kn in need:
            if know[eng].get(s, 0) >= v:
                continue
            queue[eng].wait_ge(T.sem[s], v)
            waited[s] = max(waited.get(s, 0), v)
            know[eng][s] = v
            for s2, v2 in kn.items():
                know[eng][s2] = max(know[eng].get(s2, 0), v2)
        ins = fn(eng)
        if sem is not None:
            ins.then_inc(T.sem[sem], 16)
            total[sem] = shared[sem]
            done[i] = (sem, shared[sem], dict(know[eng]))
        elif i in marked:
            s = "c" + eng
            total[s] = total.get(s, 0) + 1
            ins.then_inc(T.sem[s], 1)
            done[i] = (s, total[s], dict(know[eng]))
    for s in sorted(total):
        if waited.get(s, 0) < total[s]:
            (g.sync if s == "st" else g).wait_ge(T.sem[s], total[s])


def rank_program(g, core, T, topo):
    rank = T.rank_of(core)
    if rank is None:
        return
    n_ranks = len(T.cores)
    V, SC, PE = g.vector, g.scalar, g.tensor
    ops, bank = [], {}

    def op(name, eng, fn, r, w, sem=None):
        ops.append((name, eng, fn, r, w, sem))

    common = set.intersection(*[set(topo.engines(a, b)) for a in T.cores for b in T.cores if a != b])
    mask, ne = sum(1 << e for e in common), len(common)

    arrivals, extra = {}, {"gone": 0}
    for t in range(R):
        arrivals["LQ%d" % t] = ("rq%d" % t, 2 * ne)
        arrivals["LL%d" % t] = ("rl%d" % t, ne)
        extra["rq%d" % t] = 2 * ne
        extra["rl%d" % t] = ne

    def send(name, t, out, in_, sem, r):
        dst = T.cores[(rank + 1 + t) % n_ranks]
        rid, pid = topo.addr(dst, core)
        extra["gone"] += ne
        op(name, "G", lambda e: g.remote_dma(out, in_, T.sem[sem], T.sem.gone, pid, rid, mask), r, [])

    def load(name, out, in_, r, w, sem):
        op(name, "S", lambda e: g.sync.dma_start(out, in_), r, w, sem)

    def store(name, eng, out, in_, r):
        op(name, eng, lambda e: (g.sync if e == "S" else SC).dma_start(out, in_), r, [], "st")

    def ts(name, out, in0, s1, s2, o0, o1, r, w):
        if o1 is None:
            op(name, "V", lambda e: V.tensor_scalar(out, in0, s1, None, o0), r, w)
        else:
            op(name, "V", lambda e: V.tensor_scalar(out, in0, s1, s2, o0, o1), r, w)

    def tt(name, out, a, b, o, r, w):
        op(name, "V", lambda e: V.tensor_tensor(out, a, b, o), r, w)

    def scan(name, out, a, b, first, o0, o1, r, w):
        op(name, "V", lambda e: V.tensor_tensor_scan(out, a(), b, first, o0, o1), r, w)

    def fill(name, ap, c, w):
        op(name, "V", lambda e: V.memset(ap, c), [], w)

    def iota(name, out, pattern, base, step, w):
        op(name, "G", lambda e: g.iota(out, pattern, base, step, allow_small_or_imprecise_dtypes=True), [], w)

    def act(name, out, in_, func, r, w, **kw):
        op(name, "A", lambda e: SC.activation(out, in_, func, **kw), r, w)

    def affine(name, out, in_, scale, bias, r, w):
        col = not isinstance(bias, float)
        op(name, "AV", lambda e: V.tensor_scalar(out, in_, scale, bias, ALU.mult, ALU.add) if e == "V"
           else SC.activation(out, in_, ACT.Identity if col else ACT.Copy, scale=scale, bias=bias), r, w)

    def copy(name, eng, out, in_, r, w):
        op(name, eng, lambda e: V.tensor_copy(out, in_) if e == "V" else SC.activation(out, in_, ACT.Copy), r, w)

    def quant(name, a, b, in_, r, w):
        op("q" + w, "V", lambda e: V.quantize_mx(T["q" + name][:, a:b], T["s" + name][:, a:b], in_), r, [w])

    ps = lambda name: T["ps%d" % bank[name]]

    def mm(name, terms, r):
        def fn(e):
            ins = None
            for i, (ln, la, rn, ra, n) in enumerate(terms):
                ins = PE.matmul_mx(ps(name)[:, 0:n], T["q" + ln][:, la:la + 128], T["s" + ln][:, la:la + 128],
                                   T["q" + rn][:, ra:ra + n], T["s" + rn][:, ra:ra + n], i == 0, i == len(terms) - 1)
            return ins
        op("m" + name, "P", fn, r, ["+" + name])

    def out_of(name, eng, dst, scale, w, n=A):
        def fn(e):
            src = ps(name)[:, 0:n]
            return (V.tensor_scalar(dst, src, scale, None, ALU.mult) if e == "V"
                    else SC.activation(dst, src, ACT.Copy, scale=scale))
        op("o" + name, eng, fn, [], ["-" + name, w])

    pf = lambda j: T.pf[:, j:j + 1]
    pb = lambda j: T.pb[:, 2 * j:2 * j + 1]
    P2, S1, S2, K2, U2, KAP, TOP, LOW, THR, MINE = range(10)
    lt = lambda t: T["lt%d" % t][:] if t < R - 1 else T.lf[:, 0:2 * S:2]
    lx = lambda t: T["lx%d" % t][:] if t < R - 1 else T.lf[:, 1:2 * S:2]

    def plane(win, o):
        return T[("fa", "fb")[o]] if win == "F" else T[("wa", "wb")[o] + win]

    def product(name, win, part, terms, r):
        for b in (1, 3, 0, 2):
            mm(name + str(b), terms(b), r + ["E%d" % b])
        for b in (1, 3, 0, 2):
            if win == "F":
                first, step = FAR0 + 2 * (b >> 1) + 1, 4
            else:
                j = "tbh".index(part)
                first, step = 6 * E * j + 3 * (b >> 1) + j, 6
            out_of(name + str(b), ("VA", "AV")[b & 1], plane(win, b & 1)[:, first:first + step * (A - 1) + 1:step], SMALL,
                   win + part + str(b))

    def gather(name, tile, first, win, parts, lst, col, r, n=S):
        made = []
        for piece, eng, o, a, b in (("b", "AV", 1, 0, n), ("a", "VA", 0, 0, CUT[name]), ("c", "AV", 0, CUT[name], n)):
            if a < b:
                keys = [("" if p in parts else "?") + win + p + str(j) for p in ("tz" if win == "F" else "tbh")
                        for j in (o, o + 2)]
                copy("g" + name + piece, eng, tile[:, first + 32 * a + o:first + 32 * b:2],
                     plane(win, o)[:].indirect(lst[:, col + a:col + b]), r + keys, [name + piece])
                made.append(name + piece)
        return made

    load("ldx", T.xin[:], T.x[:], [], ["xin"], "dx")
    load("ldu", T.uin[:], T.u[:], [], ["uin"], "du")
    load("ldwc", T.qw[:].bitcast(dt.uint8), T.wc[:], ["xin"], ["qw"], "dw")
    load("ldws", T.sw[:], T.ws[:], ["xin"], ["sw"], "dw")

    base = round(24 * (FAR0 - STEP * (1 + 1120) + 640) + 13)
    iota("ip", pf(P2), [[0, 1]], 0, 2, ["p"])
    iota("ia1", T.a1[:], [[1, 24], [1, NE]], -S, -1, ["a1"])
    iota("ia2", T.a2[:], [[-1, 24], [1, NE]], S - 2, -1, ["a2"])
    iota("ijp", T.jp[:], [[1, 128]], 0, -1, ["jp"])
    iota("ivv", T.vi[:], [[-768, S], [98, NE]], base + 768 * (S - 1), 0, ["vi"])
    fill("z0", T.z0[:], 0.0, ["z0"])
    for j in (1, 2, 3):
        for name, ap, n in (("ct", T.ct[:, j:4 * NC:4], NC), ("ft", T.ft[:, j:512:4], 128),
                            ("zb", T.zb[:, j - 1:516:4], 129)):
            op("z%s%d" % (name, j), "AV", lambda e, ap=ap, n=n: V.memset(ap, 0.0) if e == "V"
               else SC.activation(ap, T.z0[:, 0:n], ACT.Copy), ["z0"], ["%s%d" % (name, j)])
    for o in (0, 1):
        ap = plane("F", o)[:, FAR0 - 4 * E:FAR0 - 4 * E + 4 * A:2]
        op("zF%d" % o, "VG", lambda e, ap=ap: V.memset(ap, 0.0) if e == "V"
           else g.iota(ap, [[0, 2 * A]], 0, 0, allow_small_or_imprecise_dtypes=True), [], ["Fz%d" % o, "Fz%d" % (o + 2)])
    fill("dd0", T.dd[:, 0:S], -32 - STEP, ["dd0"])
    fill("dd1", T.dd[:, S:2 * S], 32 - STEP, ["dd1"])
    affine("p8", pb(0), pf(P2), 0.5, 1280 - 3.5, ["p"], ["p8"])
    affine("p16", pb(1), pf(P2), 0.5, 2560 - 7.5, ["p"], ["p16"])
    affine("p2", pb(2), pf(P2), 0.5, 320 - 0.5, ["p"], ["p2"])
    affine("s1", pf(S1), pb(0), -1.125, 1440.0, ["p8"], ["s1"])
    affine("s2", pf(S2), pb(0), -0.875, 1120.0, ["p8"], ["s2"])
    affine("k2", pf(K2), pb(1), -1.0, pb(2), ["p16", "p2"], ["k2"])
    affine("u2", pf(U2), pb(2), -2.0, pf(P2), ["p2", "p"], ["u2"])
    affine("kap", pf(KAP), pf(K2), -STEP / 2, pf(U2), ["k2", "u2"], ["kap"])
    affine("vv", T.vv[:], T.vi[:], 1 / 24, pf(KAP), ["vi", "kap"], ["vv"])
    first = 6.125 * (1 + 2240) - 0.4375 - 1.5 * (FAR0 + 13 / 24)
    affine("top", pf(TOP), pf(K2), 6.125, first, ["k2"], ["top"])
    affine("low", pf(LOW), pf(K2), 6.125, first + 49, ["k2"], ["low"])
    affine("thr", pf(THR), pf(K2), -2.0, 30.0 - 2 * 2240, ["k2"], ["thr"])
    affine("mine", pf(MINE), pf(K2), -STEP, -STEP * (1 + 2240), ["k2"], ["mine"])
    affine("cown", T.cown[:], T.vv[:, NC - NE::-NE], 1.0, pf(MINE), ["vv", "mine"], ["cown"])
    ts("m1", T.m1[:], T.a1[:], pf(S1), BIG, ALU.is_ge, ALU.mult, ["a1", "s1"], ["m1"])
    ts("m2", T.m2[:], T.a2[:], pf(S2), None, ALU.is_ge, None, ["a2", "s2"], ["m2"])
    tt("m3", T.m3[:], T.m1[:], T.m2[:], ALU.mult, ["m1", "m2"], ["m3"])
    affine("ct0", T.ct[:, 0:4 * NC:4], T.m3[:, 0:NC], 1.0, 0.0, ["m3"], ["ct0"])
    affine("ct1", T.ct[96:128, 1:4 * NC:4], T.m3[96:128, 4 * NE:4 * NE + NC], 0.5, 0.0, ["m3"], ["ct1"])
    quant("c", 0, NC, T.ct[:], ["ct0", "ct1", "ct2", "ct3"], "cone")
    ts("lu", T.lu[:], T.vi[:, NC - NE:NC - NE - 8 * NE:-NE], float(-base), 16 / 768, ALU.add, ALU.mult, ["vi"], ["lu"])
    ts("zb", T.zb[:, 3:515:4], T.jp[:], 0.0, 64.0, ALU.is_equal, ALU.mult, ["jp"], ["zb0"])
    for b in range(4):
        quant("e", 128 * b, 128 * b + 128, T.zb[:, 3 - b:515 - b], ["zb0", "zb1", "zb2", "zb3"], "E%d" % b)

    copy("xtb", "AV", T.xh[:, 32 * CUT["x"]:4 * A], T.xin[:, CUT["x"]:S, 0:32], ["xin"], ["xtb"])
    copy("xta", "VA", T.xh[:, 0:32 * CUT["x"]], T.xin[:, 0:CUT["x"], 0:32], ["xin"], ["xta"])
    quant("x0", 0, A, T.xh[:, 0:4 * A], ["xta", "xtb"], "T0")
    copy("xb", "VA", T.xh[:, 4 * A:8 * A], T.xin[:, :, 32:64], ["xin"], ["xb"])
    quant("x0", A, C, T.xh[:, 4 * A:8 * A], ["xb"], "L0")
    quant("u", 0, 128, T.uin[:], ["uin"], "u0")
    op("urq", "V", lambda e: V.tensor_copy(T.qur[:].bitcast(dt.uint32), T.qu[:].bitcast(dt.uint32).indirect(T.lu[:])),
       ["u0", "lu"], ["qur"])
    copy("urs", "AV", T.sur[:], T.su[:].indirect(T.lu[:]), ["u0", "lu"], ["sur"])

    for t in range(R):
        k, n = str(t), str(t + 1)
        x, gg, lnd = "x" + k, T["g" + k], T["lnd" + k]
        rx = lambda i: T["rx" + k][:, S * i:S * i + S]
        send("sq" + k, t, T["ql" + k][:].bitcast(dt.uint8), T["q" + x][:, 0:A].bitcast(dt.uint8), "rq" + k, ["T" + k])
        send("ss" + k, t, T["sl" + k][:], T["s" + x][:, 0:A], "rq" + k, ["T" + k])
        mm("P" + k, [(x, 0, "ur", 0, 128)], ["T" + k, "qur", "sur"])
        mm("Q" + k, [(x, 32, "ur", 0, 128)], ["T" + k, "qur", "sur"])
        op("oP" + k, "V", lambda e, k=k: V.tensor_scalar(T.ft[:, 0:512:4], ps("P" + k)[:, 0:128], 0.0, 0.5, ALU.is_gt,
                                                         ALU.subtract), [], ["-P" + k, "ft0"])
        op("oQ" + k, "A", lambda e, k=k: SC.activation(T.ft[96:128, 1:512:4], ps("Q" + k)[96:128, 0:128], ACT.Sign,
                                                       bias=-2.0 ** -126), [], ["-Q" + k, "ft1"])
        quant("f" + k, 0, 128, T.ft[:], ["ft0", "ft1", "ft2", "ft3"], "f" + k)
        mm("C" + k, [("f" + k, 0, "c", 0, NC)], ["f" + k, "cone"])
        scan("oC" + k, T["d" + k][:], lambda k=k: ps("C" + k)[:, 0:NC], T.vv[:], BIG, ALU.max, ALU.min, ["vv"],
             ["-C" + k, "d" + k])
        scan("fw" + k, T["fw" + k][:], lambda: T.dd[:, 0:S], T["d" + k][:, E:NC:NE], 0.0, ALU.add, ALU.max,
             ["dd0", "d" + k], ["fw" + k])
        for name, out in (("ls" + k, T["ls" + k]), ("g" + k, gg)):
            scan(name, out[:], lambda: T.dd[:, S:2 * S], T["fw" + k][:, S - 1::-1], -BIG, ALU.add, ALU.max,
                 ["dd1", "fw" + k], [name])
        send("sg" + k, t, lnd[:], T["ls" + k][:], "rl" + k, ["ls" + k])
        product("T" + k, k, "t", lambda b: [("e", 128 * b, x, 0, A)], ["T" + k])
        product("F" + k, "F", "t", lambda b: [("e", 128 * b, "l" + k, 0, A)], ["LQ" + k])
        quant("b" + k, 0, A, T["bt" + k][:], gather("B" + k, T["bt" + k], 0, "F", "tz", lnd, 0, ["LL" + k]), "B" + k)
        product("L" + k, k, "b", lambda b: [("e", 128 * b, x, A, A)], ["L" + k])
        ts("lt" + k, lt(t), gg[:], 1.5, pf(TOP), ALU.mult, ALU.add, ["g" + k, "top"], ["lt" + k])
        ts("ra" + k, rx(0), lnd[:], pf(THR), None, ALU.add, None, ["LL" + k, "thr"], ["ra" + k])
        tt("rb" + k, rx(1), rx(0), gg[:], ALU.is_gt, ["g" + k, "ra" + k], ["rb" + k])
        tt("rc" + k, rx(2), rx(1), gg[:], ALU.mult, ["rb" + k, "g" + k], ["rc" + k])
        tt("rd" + k, rx(3), rx(2), T.cown[:], ALU.max, ["rc" + k, "cown"], ["rd" + k])
        ts("lx" + k, lx(t), rx(3), 1.5, pf(LOW), ALU.mult, ALU.add, ["rd" + k, "low"], ["lx" + k])
        if t < R - 1:
            quant("x" + n, 0, A, T["xs" + k][:, 0:4 * A],
                  gather("top" + k, T["xs" + k], 0, k, "tb", T["lt" + k], 0, ["lt" + k]), "T" + n)
        product("H" + k, k, "h", lambda b: [("w", 128 * b, "b" + k, 0, A), ("e", 128 * b, "b" + k, 0, A)],
                ["B" + k, "qw", "sw"])
        if t < R - 1:
            quant("x" + n, A, C, T["xs" + k][:, 4 * A:8 * A],
                  gather("low" + k, T["xs" + k], 4 * A, k, "tbh", T["lx" + k], 0, ["lx" + k]), "L" + n)

    load("ldv", T.vin[:], T.v[:], ["L1"], ["vin"], "dv")
    quant("v", 0, 128, T.vin[:], ["vin"], "v0")
    tt("oa0", T.oab[:, 0:S], T.g2[:], T.vv[:, NC - NE::-NE], ALU.subtract, ["g2", "vv"], ["oa0"])
    affine("oa1", T.oab[:, S:2 * S], T.oab[:, 0:S], 1 / STEP, 2.0 ** 23, ["oa0"], ["oa1"])
    affine("oa2", T.oab[:, 2 * S:3 * S], T.oab[:, S:2 * S], 1.0, -2.0 ** 23, ["oa1"], ["oa2"])
    store("stoa", "SA", T.oa[:], T.oab[0:128:16, 2 * S:3 * S], ["oa2"])
    for h, (a, b) in enumerate(((0, CUT["half"]), (CUT["half"], S))):
        k = str(h)
        quant("x3", 16 * a, 16 * b, T.xs2[:, 64 * a:64 * b],
              gather("end" + k, T.xs2, 64 * a, "2", "tbh", T.lf, 2 * a, ["lt2", "lx2"], 2 * (b - a)), "X" + k)
        mm("Y" + k, [("v", 0, "x3", 16 * a, 16 * (b - a))], ["v0", "X" + k])
        store("stc" + k, "SA", T.oc[:, 64 * a:64 * b], T.qx3[:, 16 * a:16 * b].bitcast(dt.uint8), ["X" + k])
        out_of("Y" + k, "AV", T.yb[:, a:b, :], 1.0, "yb" + k, 16 * (b - a))
        store("sty" + k, "AS", T.y[:, 16 * a:16 * b], T.yb[:, a:b, :], ["yb" + k])
    for j in range(4):
        store("sts%d" % j, "SA", T.osc[4 * j:4 * j + 4, :], T.sx3[32 * j:32 * j + 4, :], ["X0", "X1"])

    if HOOK:
        HOOK[0](ops, bank)
    by_name = {o[0]: o for o in ops}
    issue = []
    for word in ORDER.split() or [o[0] for o in ops]:
        name, eng, fn, r, w, sem = by_name.pop(word.rstrip("*"))
        issue.append((name, eng[word.endswith("*")], fn, r, w, sem))
    assert not by_name
    _schedule(g, T, issue, arrivals, extra, bank)
